import numpy as np
import ml_dtypes


def mxq(x, axis, fmt="e4m3"):
    dtype, down = {"e4m3": (ml_dtypes.float8_e4m3fn, 7), "e5m2": (ml_dtypes.float8_e5m2, 14)}[fmt]
    v = np.moveaxis(np.asarray(x, np.float32).astype(ml_dtypes.bfloat16).astype(np.float64), axis, -1)
    blocks = v.reshape(v.shape[:-1] + (-1, 32))
    amax = np.abs(blocks).max(-1, keepdims=True)
    byte = np.maximum(np.where(amax > 0, np.frexp(amax)[1] - 1 + 127, 0) - down, 1)
    scale = np.exp2(byte - 127.0)
    codes = (blocks / scale).astype(np.float32).astype(dtype).astype(np.float64)
    return np.moveaxis((codes * scale).reshape(v.shape), -1, axis)


WIDE = False


def mx_kscale(k):
    if not WIDE:
        return np.ones(k)
    levels = np.array([10, -10, 5, -5, 0])
    if k % 512:
        return np.exp2(np.random.permutation(np.resize(levels, k // 32))).repeat(32)
    a = np.empty((k // 512, 16))
    for p in range(k // 512):
        a[p, :8] = np.random.permutation(np.resize(levels, 8))
        for g in range(8):
            far = levels[np.abs(levels - a[p, g]) >= 10]
            a[p, g + 8] = far[np.random.randint(len(far))]
    return np.exp2(a.ravel()).repeat(32)


def f64(x):
    return np.asarray(x).astype(np.float64)


def striped8(idx):
    return np.concatenate([x.reshape(-1, 16).T for x in idx]).astype(np.uint16)


def runs(offs, k):
    lists = np.stack([offs[16 * r : 16 * r + 16].T.reshape(-1) for r in range(8)]).astype(np.int64)
    return lists[np.arange(k) % 512 // 64]


def pack_weight(w):
    k, n = w.shape
    w = f64(np.asarray(w, np.float32).astype(ml_dtypes.bfloat16)).reshape(k // 32, 32, n)
    amax = np.abs(w).max(1)
    byte = np.clip(np.where(amax > 0, np.frexp(amax)[1] - 1 + 127 - 7, 1), 1, 254)
    scaled = (w * np.exp2(127.0 - byte)[:, None, :]).reshape(k, n).astype(np.float32)
    words = np.ascontiguousarray(scaled.reshape(k // 512, 128, 4, n).transpose(0, 1, 3, 2)).astype(ml_dtypes.float8_e4m3fn).view(np.uint8)
    return words, np.ascontiguousarray(byte.astype(np.uint8).reshape(k // 512, 16, n))


def unpack_weight(words, scales):
    g, p, n, _ = words.shape
    vals = np.ascontiguousarray(words).view(ml_dtypes.float8_e4m3fn).astype(np.float64) * np.repeat(np.exp2(scales.astype(np.float64) - 127.0), 8, axis=1)[..., None]
    return vals.transpose(0, 1, 3, 2).reshape(g * 512, n)


K, T, S, N = 512, 2048, 512, 256


def setup_inputs():
    n = np.random.standard_normal
    s = mx_kscale(K)[:, None]
    packed_xT = pack_weight(n((K, T)) * s)
    return {
        "x_words": packed_xT[0],
        "x_scales": packed_xT[1],
        "w1": (n((K, N)) / np.sqrt(K) / s).astype(np.float32),
        "gamma": np.random.uniform(0.5, 1.5, (N, 1)).astype(np.float32),
        "res": n((N, S)).astype(np.float32),
        "offs": striped8(np.stack([np.random.permutation(T)[:S] for _ in range(8)])),
    }


def reference(x_words, x_scales, w1, gamma, res, offs):
    xq = unpack_weight(x_words, x_scales)[np.arange(K)[:, None], runs(offs, K)]
    h = (mxq(f64(w1), 0, "e4m3").T @ xq) + f64(res)
    hn = (h - h.mean(axis=1, keepdims=True)) / np.sqrt(h.var(axis=1, keepdims=True) + 1e-5)
    return f64(gamma) * hn

@@ -1,0 +1,130 @@
+from contextlib import ExitStack
+
+import concourse.mybir as mybir
+
+K, T, S, N = 512, 2048, 512, 256
+FLOPS = 2 * K * S * N
+
+F32 = mybir.dt.float32
+BF16 = mybir.dt.bfloat16
+I32 = mybir.dt.int32
+U32 = mybir.dt.uint32
+U16 = mybir.dt.uint16
+U8 = mybir.dt.uint8
+FP8X4 = mybir.dt.float8_e4m3fn_x4
+ALU = mybir.AluOpType
+ACT = mybir.ActivationFunctionType
+
+P = 128
+PACK = 4
+BLOCK_PARTS = 8
+QUADRANT = 32
+EPS = 1e-5
+PIECES = 2
+
+
+def tile_picked_phnorm_none_p_kernel(tc, x_words, x_scales, w1, gamma, res, offs, out):
+    nc = tc.nc
+    tiles = N // P
+    width = S // PIECES
+    with ExitStack() as ctx:
+        keep = ctx.enter_context(tc.tile_pool(name="keep", bufs=1))
+        psum = ctx.enter_context(tc.psum_pool(name="psum", bufs=1))
+
+        offsets = keep.tile([P, S // 16], U16, name="offsets")
+        nc.sync.dma_start(offsets[:], offs)
+
+        scale_table = keep.tile([P, T], U8, name="scale_table", tag="table_then_res", align_bytes=64)
+        nc.vector.memset(scale_table[:].bitcast(I32), 0)
+        nc.sync.dma_start(scale_table[0:P:BLOCK_PARTS, :].bitcast(I32), x_scales[0].bitcast(I32))
+
+        word_table = keep.tile([P, T], I32, name="word_table", align_bytes=64)
+        w_raw = keep.tile([P, PACK, N], F32, name="w_raw")
+        nc.scalar.dma_start(w_raw[:], w1.rearrange("(p j) m -> p j m", j=PACK))
+        nc.scalar.dma_start(word_table[:], x_words[0].rearrange("p n t -> p (n t)").bitcast(I32))
+        gamma_sb = keep.tile([P, tiles], F32, name="gamma_sb")
+        with nc.allow_non_contiguous_dma(reason="one value a channel"):
+            nc.sync.dma_start(gamma_sb[:], gamma.rearrange("(c p) o -> p (c o)", p=P))
+
+        warm = keep.tile([P, 2], F32, name="warm")
+        nc.vector.memset(warm[:, 0:1], 1.0)
+        nc.scalar.activation(out=warm[:, 1:2], in_=warm[:, 0:1], func=ACT.Abs_reciprocal_sqrt)
+
+        x_scale = keep.tile([P, S], U8, name="x_scale", align_bytes=64)
+        nc.vector.memset(x_scale[:].bitcast(I32), 0)
+        picked_scales = keep.tile([P, S], U8, name="picked_scales", align_bytes=64)
+        nc.vector.tensor_copy(picked_scales[:], scale_table[:].indirect(offsets[:]))
+        for i in range(QUADRANT // BLOCK_PARTS):
+            nc.sync.dma_start(
+                x_scale[i:P:QUADRANT, :].bitcast(I32),
+                picked_scales[BLOCK_PARTS * i : P : QUADRANT, :].bitcast(I32),
+            )
+        res_all = keep.tile([P, tiles, S], F32, name="res_all", tag="table_then_res", align_bytes=64)
+        nc.sync.dma_start(res_all[:], res.rearrange("(c p) s -> p c s", p=P))
+        res_sb = [res_all[:, c, :] for c in range(tiles)]
+
+        w_ops = []
+        for c in range(tiles):
+            grouped = keep.tile([P, P, PACK], BF16, name=f"grouped{c}", align_bytes=64)
+            source = w_raw[:, :, c * P : (c + 1) * P].rearrange("p j m -> p m j")
+            if c < 0:
+                nc.vector.tensor_copy(out=grouped[:], in_=source)
+            else:
+                nc.scalar.copy(out=grouped[:], in_=source)
+            w_codes = keep.tile([P, P], U32, name=f"w_codes{c}", align_bytes=64)
+            w_scale = keep.tile([P, P], U8, name=f"w_scale{c}", align_bytes=64)
+            nc.vector.quantize_mx(
+                out=w_codes[:].bitcast(FP8X4),
+                scales=w_scale[:],
+                in_=grouped[:].rearrange("p m j -> p (m j)"),
+            )
+            w_ops.append((w_codes, w_scale))
+
+        accs = [psum.tile([P, S], F32, name=f"acc{c}") for c in range(tiles)]
+        x_codes = keep.tile([P, S], U32, name="x_codes", align_bytes=64)
+        for u in range(PIECES):
+            cols = slice(u * width, (u + 1) * width)
+            entries = offsets[:, u * width // 16 : (u + 1) * width // 16]
+            nc.vector.tensor_copy(x_codes[:, cols], word_table[:].bitcast(U32).indirect(entries))
+            for c in range(tiles):
+                nc.tensor.matmul_mx(
+                    out=accs[c][:, cols],
+                    lhsT=w_ops[c][0][:].bitcast(FP8X4),
+                    lhsT_scale=w_ops[c][1][:],
+                    rhs=x_codes[:, cols].bitcast(FP8X4),
+                    rhs_scale=x_scale[:, cols],
+                    start=True,
+                    stop=True,
+                )
+
+        for c in range(tiles):
+            h = keep.tile([P, S], F32, name=f"h{c}")
+            total = keep.tile([P, 1], F32, name=f"total{c}")
+            nc.vector.scalar_tensor_tensor(
+                out=h[:], in0=accs[c][:], scalar=1.0, in1=res_sb[c],
+                op0=ALU.mult, op1=ALU.add, accum_out=total[:],
+            )
+            squares = keep.tile([P, S], F32, name=f"squares{c}")
+            spread = keep.tile([P, 1], F32, name=f"spread{c}")
+            nc.scalar.activation(
+                out=squares[:], in_=h[:], func=ACT.Square, scale=-float(S), bias=total[:],
+                accum_out=spread[:],
+            )
+            rstd = keep.tile([P, 1], F32, name=f"rstd{c}")
+            nc.scalar.activation(
+                out=rstd[:], in_=spread[:], func=ACT.Abs_reciprocal_sqrt, scale=1.0 / S**3, bias=EPS,
+            )
+            mean = keep.tile([P, 1], F32, name=f"mean{c}")
+            nc.vector.tensor_scalar(
+                out=mean[:], in0=total[:], scalar1=1.0 / S, scalar2=None, op0=ALU.mult,
+            )
+            centred = keep.tile([P, S], F32, name=f"centred{c}")
+            nc.vector.tensor_scalar(
+                out=centred[:], in0=h[:], scalar1=mean[:], scalar2=gamma_sb[:, c : c + 1],
+                op0=ALU.subtract, op1=ALU.mult,
+            )
+            result = keep.tile([P, S], F32, name=f"result{c}")
+            nc.vector.tensor_scalar(
+                out=result[:], in0=centred[:], scalar1=rstd[:], scalar2=None, op0=ALU.mult,
+            )
+            nc.sync.dma_start(out[c * P : (c + 1) * P, :], result[:])

@@ -20,7 +20,7 @@ PACK = 4
 BLOCK_PARTS = 8
 QUADRANT = 32
 EPS = 1e-5
-PIECES = 2
+PIECES = 1
 
 
 def tile_picked_phnorm_none_p_kernel(tc, x_words, x_scales, w1, gamma, res, offs, out):
@@ -35,16 +35,16 @@ def tile_picked_phnorm_none_p_kernel(tc, x_words, x_scales, w1, gamma, res, offs
         nc.sync.dma_start(offsets[:], offs)
 
         scale_table = keep.tile([P, T], U8, name="scale_table", tag="table_then_res", align_bytes=64)
-        nc.vector.memset(scale_table[:].bitcast(I32), 0)
-        nc.sync.dma_start(scale_table[0:P:BLOCK_PARTS, :].bitcast(I32), x_scales[0].bitcast(I32))
+        rows = x_scales[0].bitcast(I32).unsqueeze(1).to_broadcast([P // BLOCK_PARTS, BLOCK_PARTS, T // 4])
+        nc.sync.dma_start(scale_table[:].bitcast(I32), rows)
 
         word_table = keep.tile([P, T], I32, name="word_table", align_bytes=64)
         w_raw = keep.tile([P, PACK, N], F32, name="w_raw")
-        nc.scalar.dma_start(w_raw[:], w1.rearrange("(p j) m -> p j m", j=PACK))
-        nc.scalar.dma_start(word_table[:], x_words[0].rearrange("p n t -> p (n t)").bitcast(I32))
+        nc.sync.dma_start(word_table[:], x_words[0].rearrange("p n t -> p (n t)").bitcast(I32))
+        nc.sync.dma_start(w_raw[:], w1.rearrange("(p j) m -> p j m", j=PACK))
         gamma_sb = keep.tile([P, tiles], F32, name="gamma_sb")
         with nc.allow_non_contiguous_dma(reason="one value a channel"):
-            nc.sync.dma_start(gamma_sb[:], gamma.rearrange("(c p) o -> p (c o)", p=P))
+            nc.gpsimd.dma_start(gamma_sb[:], gamma.rearrange("(c p) o -> p (c o)", p=P))
 
         warm = keep.tile([P, 2], F32, name="warm")
         nc.vector.memset(warm[:, 0:1], 1.0)
@@ -55,7 +55,8 @@ def tile_picked_phnorm_none_p_kernel(tc, x_words, x_scales, w1, gamma, res, offs
         picked_scales = keep.tile([P, S], U8, name="picked_scales", align_bytes=64)
         nc.vector.tensor_copy(picked_scales[:], scale_table[:].indirect(offsets[:]))
         for i in range(QUADRANT // BLOCK_PARTS):
-            nc.sync.dma_start(
+            queue = nc.scalar if i % 2 == 0 else nc.sync
+            queue.dma_start(
                 x_scale[i:P:QUADRANT, :].bitcast(I32),
                 picked_scales[BLOCK_PARTS * i : P : QUADRANT, :].bitcast(I32),
             )
@@ -67,7 +68,7 @@ def tile_picked_phnorm_none_p_kernel(tc, x_words, x_scales, w1, gamma, res, offs
         for c in range(tiles):
             grouped = keep.tile([P, P, PACK], BF16, name=f"grouped{c}", align_bytes=64)
             source = w_raw[:, :, c * P : (c + 1) * P].rearrange("p j m -> p m j")
-            if c < 0:
+            if c < 1:
                 nc.vector.tensor_copy(out=grouped[:], in_=source)
             else:
                 nc.scalar.copy(out=grouped[:], in_=source)
@@ -112,19 +113,16 @@ def tile_picked_phnorm_none_p_kernel(tc, x_words, x_scales, w1, gamma, res, offs
             )
             rstd = keep.tile([P, 1], F32, name=f"rstd{c}")
             nc.scalar.activation(
-                out=rstd[:], in_=spread[:], func=ACT.Abs_reciprocal_sqrt, scale=1.0 / S**3, bias=EPS,
-            )
-            mean = keep.tile([P, 1], F32, name=f"mean{c}")
-            nc.vector.tensor_scalar(
-                out=mean[:], in0=total[:], scalar1=1.0 / S, scalar2=None, op0=ALU.mult,
+                out=rstd[:], in_=spread[:], func=ACT.Abs_reciprocal_sqrt, scale=1.0 / S, bias=EPS * S * S,
             )
             centred = keep.tile([P, S], F32, name=f"centred{c}")
             nc.vector.tensor_scalar(
-                out=centred[:], in0=h[:], scalar1=mean[:], scalar2=gamma_sb[:, c : c + 1],
-                op0=ALU.subtract, op1=ALU.mult,
+                out=centred[:], in0=h[:], scalar1=float(S), scalar2=total[:],
+                op0=ALU.mult, op1=ALU.subtract,
             )
             result = keep.tile([P, S], F32, name=f"result{c}")
             nc.vector.tensor_scalar(
-                out=result[:], in0=centred[:], scalar1=rstd[:], scalar2=None, op0=ALU.mult,
+                out=result[:], in0=centred[:], scalar1=rstd[:], scalar2=gamma_sb[:, c : c + 1],
+                op0=ALU.mult, op1=ALU.mult,
             )
             nc.sync.dma_start(out[c * P : (c + 1) * P, :], result[:])

@@ -35,16 +35,15 @@ def tile_picked_phnorm_none_p_kernel(tc, x_words, x_scales, w1, gamma, res, offs
         nc.sync.dma_start(offsets[:], offs)
 
         scale_table = keep.tile([P, T], U8, name="scale_table", tag="table_then_res", align_bytes=64)
-        rows = x_scales[0].bitcast(I32).unsqueeze(1).to_broadcast([P // BLOCK_PARTS, BLOCK_PARTS, T // 4])
-        nc.sync.dma_start(scale_table[:].bitcast(I32), rows)
-
-        word_table = keep.tile([P, T], I32, name="word_table", align_bytes=64)
+        nc.vector.memset(scale_table[:, : T // 2].bitcast(I32), 0)
+        nc.gpsimd.memset(scale_table[:, T // 2 :].bitcast(I32), 0)
         w_raw = keep.tile([P, PACK, N], F32, name="w_raw")
+        w_rows = w1.rearrange("(p j) m -> p j m", j=PACK)
+        nc.sync.dma_start(w_raw[:, : PACK // 2, :], w_rows[:, : PACK // 2, :])
+        nc.sync.dma_start(scale_table[0:P:BLOCK_PARTS, :].bitcast(I32), x_scales[0].bitcast(I32))
+        word_table = keep.tile([P, T], I32, name="word_table", align_bytes=64)
         nc.sync.dma_start(word_table[:], x_words[0].rearrange("p n t -> p (n t)").bitcast(I32))
-        nc.sync.dma_start(w_raw[:], w1.rearrange("(p j) m -> p j m", j=PACK))
-        gamma_sb = keep.tile([P, tiles], F32, name="gamma_sb")
-        with nc.allow_non_contiguous_dma(reason="one value a channel"):
-            nc.gpsimd.dma_start(gamma_sb[:], gamma.rearrange("(c p) o -> p (c o)", p=P))
+        nc.sync.dma_start(w_raw[:, PACK // 2 :, :], w_rows[:, PACK // 2 :, :])
 
         warm = keep.tile([P, 2], F32, name="warm")
         nc.vector.memset(warm[:, 0:1], 1.0)
@@ -60,9 +59,13 @@ def tile_picked_phnorm_none_p_kernel(tc, x_words, x_scales, w1, gamma, res, offs
                 x_scale[i:P:QUADRANT, :].bitcast(I32),
                 picked_scales[BLOCK_PARTS * i : P : QUADRANT, :].bitcast(I32),
             )
-        res_all = keep.tile([P, tiles, S], F32, name="res_all", tag="table_then_res", align_bytes=64)
-        nc.sync.dma_start(res_all[:], res.rearrange("(c p) s -> p c s", p=P))
+        late = keep.tile([P, tiles * S + tiles], F32, name="late", tag="table_then_res", align_bytes=64)
+        res_all = late[:, : tiles * S].rearrange("p (c s) -> p c s", c=tiles)
+        nc.sync.dma_start(res_all, res.rearrange("(c p) s -> p c s", p=P))
         res_sb = [res_all[:, c, :] for c in range(tiles)]
+        gamma_sb = late[:, tiles * S :]
+        with nc.allow_non_contiguous_dma(reason="one value a channel"):
+            nc.sync.dma_start(gamma_sb, gamma.rearrange("(c p) o -> p (c o)", p=P))
 
         w_ops = []
         for c in range(tiles):

@@ -20,7 +20,7 @@ PACK = 4
 BLOCK_PARTS = 8
 QUADRANT = 32
 EPS = 1e-5
-PIECES = 1
+PIECES = 2
 
 
 def tile_picked_phnorm_none_p_kernel(tc, x_words, x_scales, w1, gamma, res, offs, out):
@@ -41,9 +41,9 @@ def tile_picked_phnorm_none_p_kernel(tc, x_words, x_scales, w1, gamma, res, offs
         w_rows = w1.rearrange("(p j) m -> p j m", j=PACK)
         nc.sync.dma_start(w_raw[:, : PACK // 2, :], w_rows[:, : PACK // 2, :])
         nc.sync.dma_start(scale_table[0:P:BLOCK_PARTS, :].bitcast(I32), x_scales[0].bitcast(I32))
+        nc.sync.dma_start(w_raw[:, PACK // 2 :, :], w_rows[:, PACK // 2 :, :])
         word_table = keep.tile([P, T], I32, name="word_table", align_bytes=64)
         nc.sync.dma_start(word_table[:], x_words[0].rearrange("p n t -> p (n t)").bitcast(I32))
-        nc.sync.dma_start(w_raw[:, PACK // 2 :, :], w_rows[:, PACK // 2 :, :])
 
         warm = keep.tile([P, 2], F32, name="warm")
         nc.vector.memset(warm[:, 0:1], 1.0)
@@ -67,22 +67,15 @@ def tile_picked_phnorm_none_p_kernel(tc, x_words, x_scales, w1, gamma, res, offs
         with nc.allow_non_contiguous_dma(reason="one value a channel"):
             nc.sync.dma_start(gamma_sb, gamma.rearrange("(c p) o -> p (c o)", p=P))
 
-        w_ops = []
-        for c in range(tiles):
-            grouped = keep.tile([P, P, PACK], BF16, name=f"grouped{c}", align_bytes=64)
-            source = w_raw[:, :, c * P : (c + 1) * P].rearrange("p j m -> p m j")
-            if c < 1:
-                nc.vector.tensor_copy(out=grouped[:], in_=source)
-            else:
-                nc.scalar.copy(out=grouped[:], in_=source)
-            w_codes = keep.tile([P, P], U32, name=f"w_codes{c}", align_bytes=64)
-            w_scale = keep.tile([P, P], U8, name=f"w_scale{c}", align_bytes=64)
-            nc.vector.quantize_mx(
-                out=w_codes[:].bitcast(FP8X4),
-                scales=w_scale[:],
-                in_=grouped[:].rearrange("p m j -> p (m j)"),
-            )
-            w_ops.append((w_codes, w_scale))
+        grouped = keep.tile([P, N, PACK], BF16, name="grouped", align_bytes=64)
+        nc.vector.tensor_copy(out=grouped[:], in_=w_raw[:].rearrange("p j m -> p m j"))
+        w_codes = keep.tile([P, N], U32, name="w_codes", align_bytes=64)
+        w_scale = keep.tile([P, N], U8, name="w_scale", align_bytes=64)
+        nc.vector.quantize_mx(
+            out=w_codes[:].bitcast(FP8X4),
+            scales=w_scale[:],
+            in_=grouped[:].rearrange("p m j -> p (m j)"),
+        )
 
         accs = [psum.tile([P, S], F32, name=f"acc{c}") for c in range(tiles)]
         x_codes = keep.tile([P, S], U32, name="x_codes", align_bytes=64)
@@ -90,11 +83,13 @@ def tile_picked_phnorm_none_p_kernel(tc, x_words, x_scales, w1, gamma, res, offs
             cols = slice(u * width, (u + 1) * width)
             entries = offsets[:, u * width // 16 : (u + 1) * width // 16]
             nc.vector.tensor_copy(x_codes[:, cols], word_table[:].bitcast(U32).indirect(entries))
-            for c in range(tiles):
+        for c in range(tiles):
+            for u in range(PIECES):
+                cols = slice(u * width, (u + 1) * width)
                 nc.tensor.matmul_mx(
                     out=accs[c][:, cols],
-                    lhsT=w_ops[c][0][:].bitcast(FP8X4),
-                    lhsT_scale=w_ops[c][1][:],
+                    lhsT=w_codes[:, c * P : (c + 1) * P].bitcast(FP8X4),
+                    lhsT_scale=w_scale[:, c * P : (c + 1) * P],
                     rhs=x_codes[:, cols].bitcast(FP8X4),
                     rhs_scale=x_scale[:, cols],
                     start=True,

@@ -45,6 +45,9 @@ def tile_picked_phnorm_none_p_kernel(tc, x_words, x_scales, w1, gamma, res, offs
         word_table = keep.tile([P, T], I32, name="word_table", align_bytes=64)
         nc.sync.dma_start(word_table[:], x_words[0].rearrange("p n t -> p (n t)").bitcast(I32))
 
+        res_first = keep.tile([P, S], F32, name="res_first")
+        nc.sync.dma_start(res_first[:], res[0:P, :])
+
         warm = keep.tile([P, 2], F32, name="warm")
         nc.vector.memset(warm[:, 0:1], 1.0)
         nc.scalar.activation(out=warm[:, 1:2], in_=warm[:, 0:1], func=ACT.Abs_reciprocal_sqrt)
@@ -59,11 +62,10 @@ def tile_picked_phnorm_none_p_kernel(tc, x_words, x_scales, w1, gamma, res, offs
                 x_scale[i:P:QUADRANT, :].bitcast(I32),
                 picked_scales[BLOCK_PARTS * i : P : QUADRANT, :].bitcast(I32),
             )
-        late = keep.tile([P, tiles * S + tiles], F32, name="late", tag="table_then_res", align_bytes=64)
-        res_all = late[:, : tiles * S].rearrange("p (c s) -> p c s", c=tiles)
-        nc.sync.dma_start(res_all, res.rearrange("(c p) s -> p c s", p=P))
-        res_sb = [res_all[:, c, :] for c in range(tiles)]
-        gamma_sb = late[:, tiles * S :]
+        late = keep.tile([P, S + tiles], F32, name="late", tag="table_then_res", align_bytes=64)
+        nc.sync.dma_start(late[:, :S], res[P : 2 * P, :])
+        res_sb = [res_first[:], late[:, :S]]
+        gamma_sb = late[:, S:]
         with nc.allow_non_contiguous_dma(reason="one value a channel"):
             nc.sync.dma_start(gamma_sb, gamma.rearrange("(c p) o -> p (c o)", p=P))
 
@@ -77,17 +79,16 @@ def tile_picked_phnorm_none_p_kernel(tc, x_words, x_scales, w1, gamma, res, offs
             in_=grouped[:].rearrange("p m j -> p (m j)"),
         )
 
-        accs = [psum.tile([P, S], F32, name=f"acc{c}") for c in range(tiles)]
+        accs = [[psum.tile([P, S], F32, name=f"acc{c}_{u}") for u in range(PIECES)] for c in range(tiles)]
         x_codes = keep.tile([P, S], U32, name="x_codes", align_bytes=64)
-        for u in range(PIECES):
-            cols = slice(u * width, (u + 1) * width)
+        pieces = [slice(u * width, (u + 1) * width) for u in range(PIECES)]
+        for u, cols in enumerate(pieces):
             entries = offsets[:, u * width // 16 : (u + 1) * width // 16]
             nc.vector.tensor_copy(x_codes[:, cols], word_table[:].bitcast(U32).indirect(entries))
-        for c in range(tiles):
-            for u in range(PIECES):
-                cols = slice(u * width, (u + 1) * width)
+        for u, cols in enumerate(pieces):
+            for c in range(tiles):
                 nc.tensor.matmul_mx(
-                    out=accs[c][:, cols],
+                    out=accs[c][u][:, :width],
                     lhsT=w_codes[:, c * P : (c + 1) * P].bitcast(FP8X4),
                     lhsT_scale=w_scale[:, c * P : (c + 1) * P],
                     rhs=x_codes[:, cols].bitcast(FP8X4),
@@ -96,31 +97,50 @@ def tile_picked_phnorm_none_p_kernel(tc, x_words, x_scales, w1, gamma, res, offs
                     stop=True,
                 )
 
+        extra = width // 2
+        unit = 1.0 / (width * width * S)
+        h = [keep.tile([P, S + extra], F32, name=f"h{c}") for c in range(tiles)]
+        sums = [[keep.tile([P, 1], F32, name=f"sum{c}_{u}") for u in range(PIECES)] for c in range(tiles)]
+        spread = [[keep.tile([P, 1], F32, name=f"spread{c}_{u}") for u in range(PIECES)] for c in range(tiles)]
+        squares = keep.tile([P, tiles, S + extra], F32, name="squares")
+        base = [keep.tile([P, 1], F32, name=f"base{c}") for c in range(tiles)]
+        mean = [keep.tile([P, 1], F32, name=f"mean{c}") for c in range(tiles)]
+        rstd = [keep.tile([P, 1], F32, name=f"rstd{c}") for c in range(tiles)]
+        for u, cols in enumerate(pieces):
+            for c in range(tiles):
+                nc.vector.scalar_tensor_tensor(
+                    out=h[c][:, cols], in0=accs[c][u][:, :width], scalar=1.0, in1=res_sb[c][:, cols],
+                    op0=ALU.mult, op1=ALU.add, accum_out=sums[c][u][:],
+                )
+                span = cols if u == 0 else slice(width, S + extra)
+                nc.scalar.activation(
+                    out=squares[:, c, span], in_=h[c][:, span], func=ACT.Square, scale=-float(width),
+                    bias=sums[c][u][:], accum_out=spread[c][u][:],
+                )
+                if u == 0:
+                    nc.gpsimd.tensor_scalar(
+                        out=h[c][:, S:], in0=sums[c][0][:].to_broadcast([P, extra]), scalar1=1.0 / width,
+                        scalar2=0.0, op0=ALU.mult, op1=ALU.add,
+                    )
+                    nc.gpsimd.tensor_scalar(
+                        out=base[c][:], in0=spread[c][0][:], scalar1=unit, scalar2=EPS, op0=ALU.mult, op1=ALU.add,
+                    )
+                else:
+                    nc.vector.tensor_scalar(
+                        out=mean[c][:], in0=sums[c][0][:], scalar1=sums[c][1][:], scalar2=1.0 / S,
+                        op0=ALU.add, op1=ALU.mult,
+                    )
+                    nc.scalar.activation(
+                        out=rstd[c][:], in_=spread[c][1][:], func=ACT.Abs_reciprocal_sqrt, scale=unit, bias=base[c][:],
+                    )
         for c in range(tiles):
-            h = keep.tile([P, S], F32, name=f"h{c}")
-            total = keep.tile([P, 1], F32, name=f"total{c}")
-            nc.vector.scalar_tensor_tensor(
-                out=h[:], in0=accs[c][:], scalar=1.0, in1=res_sb[c],
-                op0=ALU.mult, op1=ALU.add, accum_out=total[:],
-            )
-            squares = keep.tile([P, S], F32, name=f"squares{c}")
-            spread = keep.tile([P, 1], F32, name=f"spread{c}")
-            nc.scalar.activation(
-                out=squares[:], in_=h[:], func=ACT.Square, scale=-float(S), bias=total[:],
-                accum_out=spread[:],
-            )
-            rstd = keep.tile([P, 1], F32, name=f"rstd{c}")
-            nc.scalar.activation(
-                out=rstd[:], in_=spread[:], func=ACT.Abs_reciprocal_sqrt, scale=1.0 / S, bias=EPS * S * S,
-            )
             centred = keep.tile([P, S], F32, name=f"centred{c}")
             nc.vector.tensor_scalar(
-                out=centred[:], in0=h[:], scalar1=float(S), scalar2=total[:],
-                op0=ALU.mult, op1=ALU.subtract,
+                out=centred[:], in0=h[c][:, :S], scalar1=mean[c][:], scalar2=gamma_sb[:, c : c + 1],
+                op0=ALU.subtract, op1=ALU.mult,
             )
             result = keep.tile([P, S], F32, name=f"result{c}")
             nc.vector.tensor_scalar(
-                out=result[:], in0=centred[:], scalar1=rstd[:], scalar2=gamma_sb[:, c : c + 1],
-                op0=ALU.mult, op1=ALU.mult,
+                out=result[:], in0=centred[:], scalar1=rstd[c][:], scalar2=None, op0=ALU.mult,
             )
             nc.sync.dma_start(out[c * P : (c + 1) * P, :], result[:])

@@ -37,24 +37,35 @@ def tile_picked_phnorm_none_p_kernel(tc, x_words, x_scales, w1, gamma, res, offs
         scale_table = keep.tile([P, T], U8, name="scale_table", tag="table_then_res", align_bytes=64)
         nc.vector.memset(scale_table[:, : T // 2].bitcast(I32), 0)
         nc.gpsimd.memset(scale_table[:, T // 2 :].bitcast(I32), 0)
-        w_raw = keep.tile([P, PACK, N], F32, name="w_raw")
         w_rows = w1.rearrange("(p j) m -> p j m", j=PACK)
-        nc.sync.dma_start(w_raw[:, : PACK // 2, :], w_rows[:, : PACK // 2, :])
+        w_raw = [keep.tile([P, PACK, P], F32, name=f"w_raw{c}", tag=f"w_raw{c}") for c in range(tiles)]
+        nc.sync.dma_start(w_raw[0][:], w_rows[:, :, 0:P])
         nc.sync.dma_start(scale_table[0:P:BLOCK_PARTS, :].bitcast(I32), x_scales[0].bitcast(I32))
-        nc.sync.dma_start(w_raw[:, PACK // 2 :, :], w_rows[:, PACK // 2 :, :])
         word_table = keep.tile([P, T], I32, name="word_table", align_bytes=64)
         nc.sync.dma_start(word_table[:], x_words[0].rearrange("p n t -> p (n t)").bitcast(I32))
-
-        res_first = keep.tile([P, S], F32, name="res_first")
-        nc.sync.dma_start(res_first[:], res[0:P, :])
+        nc.sync.dma_start(w_raw[1][:], w_rows[:, :, P : 2 * P])
 
         warm = keep.tile([P, 2], F32, name="warm")
         nc.vector.memset(warm[:, 0:1], 1.0)
         nc.scalar.activation(out=warm[:, 1:2], in_=warm[:, 0:1], func=ACT.Abs_reciprocal_sqrt)
 
+        grouped = [keep.tile([P, P, PACK], BF16, name=f"grouped{c}", align_bytes=64) for c in range(tiles)]
+        w_codes = keep.tile([P, N], U32, name="w_codes", align_bytes=64)
+        w_scale = keep.tile([P, N], U8, name="w_scale", align_bytes=64)
+
+        def quantize(c):
+            nc.vector.quantize_mx(
+                out=w_codes[:, c * P : (c + 1) * P].bitcast(FP8X4),
+                scales=w_scale[:, c * P : (c + 1) * P],
+                in_=grouped[c][:].rearrange("p m j -> p (m j)"),
+            )
+
         x_scale = keep.tile([P, S], U8, name="x_scale", align_bytes=64)
-        nc.vector.memset(x_scale[:].bitcast(I32), 0)
         picked_scales = keep.tile([P, S], U8, name="picked_scales", align_bytes=64)
+        pieces = [slice(u * width, (u + 1) * width) for u in range(PIECES)]
+        entries = [offsets[:, u * width // 16 : (u + 1) * width // 16] for u in range(PIECES)]
+        nc.vector.memset(x_scale[:].bitcast(I32), 0)
+        nc.scalar.copy(out=grouped[0][:], in_=w_raw[0][:].rearrange("p j m -> p m j"))
         nc.vector.tensor_copy(picked_scales[:], scale_table[:].indirect(offsets[:]))
         for i in range(QUADRANT // BLOCK_PARTS):
             queue = nc.scalar if i % 2 == 0 else nc.sync
@@ -62,31 +73,25 @@ def tile_picked_phnorm_none_p_kernel(tc, x_words, x_scales, w1, gamma, res, offs
                 x_scale[i:P:QUADRANT, :].bitcast(I32),
                 picked_scales[BLOCK_PARTS * i : P : QUADRANT, :].bitcast(I32),
             )
-        late = keep.tile([P, S + tiles], F32, name="late", tag="table_then_res", align_bytes=64)
-        nc.sync.dma_start(late[:, :S], res[P : 2 * P, :])
-        res_sb = [res_first[:], late[:, :S]]
-        gamma_sb = late[:, S:]
+        quantize(0)
+        late = keep.tile([P, tiles * S + tiles], F32, name="late", tag="table_then_res", align_bytes=64)
+        res_sb = [late[:, c * S : (c + 1) * S] for c in range(tiles)]
+        for cols in pieces:
+            nc.sync.dma_start(res_sb[0][:, cols], res[0:P, cols])
+        nc.sync.dma_start(res_sb[1], res[P : 2 * P, :])
+        gamma_sb = late[:, tiles * S :]
         with nc.allow_non_contiguous_dma(reason="one value a channel"):
             nc.sync.dma_start(gamma_sb, gamma.rearrange("(c p) o -> p (c o)", p=P))
 
-        grouped = keep.tile([P, N, PACK], BF16, name="grouped", align_bytes=64)
-        nc.vector.tensor_copy(out=grouped[:], in_=w_raw[:].rearrange("p j m -> p m j"))
-        w_codes = keep.tile([P, N], U32, name="w_codes", align_bytes=64)
-        w_scale = keep.tile([P, N], U8, name="w_scale", align_bytes=64)
-        nc.vector.quantize_mx(
-            out=w_codes[:].bitcast(FP8X4),
-            scales=w_scale[:],
-            in_=grouped[:].rearrange("p m j -> p (m j)"),
-        )
+        nc.scalar.copy(out=grouped[1][:], in_=w_raw[1][:].rearrange("p j m -> p m j"))
 
         accs = [[psum.tile([P, S], F32, name=f"acc{c}_{u}") for u in range(PIECES)] for c in range(tiles)]
         x_codes = keep.tile([P, S], U32, name="x_codes", align_bytes=64)
-        pieces = [slice(u * width, (u + 1) * width) for u in range(PIECES)]
         for u, cols in enumerate(pieces):
-            entries = offsets[:, u * width // 16 : (u + 1) * width // 16]
-            nc.vector.tensor_copy(x_codes[:, cols], word_table[:].bitcast(U32).indirect(entries))
-        for u, cols in enumerate(pieces):
-            for c in range(tiles):
+            nc.vector.tensor_copy(x_codes[:, cols], word_table[:].bitcast(U32).indirect(entries[u]))
+        quantize(1)
+        for c in range(tiles):
+            for u, cols in enumerate(pieces):
                 nc.tensor.matmul_mx(
                     out=accs[c][u][:, :width],
                     lhsT=w_codes[:, c * P : (c + 1) * P].bitcast(FP8X4),
@@ -106,8 +111,8 @@ def tile_picked_phnorm_none_p_kernel(tc, x_words, x_scales, w1, gamma, res, offs
         base = [keep.tile([P, 1], F32, name=f"base{c}") for c in range(tiles)]
         mean = [keep.tile([P, 1], F32, name=f"mean{c}") for c in range(tiles)]
         rstd = [keep.tile([P, 1], F32, name=f"rstd{c}") for c in range(tiles)]
-        for u, cols in enumerate(pieces):
-            for c in range(tiles):
+        for c in range(tiles):
+            for u, cols in enumerate(pieces):
                 nc.vector.scalar_tensor_tensor(
                     out=h[c][:, cols], in0=accs[c][u][:, :width], scalar=1.0, in1=res_sb[c][:, cols],
                     op0=ALU.mult, op1=ALU.add, accum_out=sums[c][u][:],
@@ -139,8 +144,9 @@ def tile_picked_phnorm_none_p_kernel(tc, x_words, x_scales, w1, gamma, res, offs
                 out=centred[:], in0=h[c][:, :S], scalar1=mean[c][:], scalar2=gamma_sb[:, c : c + 1],
                 op0=ALU.subtract, op1=ALU.mult,
             )
-            result = keep.tile([P, S], F32, name=f"result{c}")
-            nc.vector.tensor_scalar(
-                out=result[:], in0=centred[:], scalar1=rstd[c][:], scalar2=None, op0=ALU.mult,
-            )
-            nc.sync.dma_start(out[c * P : (c + 1) * P, :], result[:])
+            for u, cols in enumerate(pieces if c == tiles - 1 else [slice(0, S)]):
+                result = keep.tile([P, cols.stop - cols.start], F32, name=f"result{c}_{u}")
+                nc.vector.tensor_scalar(
+                    out=result[:], in0=centred[:, cols], scalar1=rstd[c][:], scalar2=None, op0=ALU.mult,
+                )
+                nc.sync.dma_start(out[c * P : (c + 1) * P, cols], result[:])

@@ -35,8 +35,7 @@ def tile_picked_phnorm_none_p_kernel(tc, x_words, x_scales, w1, gamma, res, offs
         nc.sync.dma_start(offsets[:], offs)
 
         scale_table = keep.tile([P, T], U8, name="scale_table", tag="table_then_res", align_bytes=64)
-        nc.vector.memset(scale_table[:, : T // 2].bitcast(I32), 0)
-        nc.gpsimd.memset(scale_table[:, T // 2 :].bitcast(I32), 0)
+        nc.vector.memset(scale_table[:].bitcast(I32), 0)
         w_rows = w1.rearrange("(p j) m -> p j m", j=PACK)
         w_raw = [keep.tile([P, PACK, P], F32, name=f"w_raw{c}", tag=f"w_raw{c}") for c in range(tiles)]
         nc.sync.dma_start(w_raw[0][:], w_rows[:, :, 0:P])
@@ -53,6 +52,12 @@ def tile_picked_phnorm_none_p_kernel(tc, x_words, x_scales, w1, gamma, res, offs
         w_codes = keep.tile([P, N], U32, name="w_codes", align_bytes=64)
         w_scale = keep.tile([P, N], U8, name="w_scale", align_bytes=64)
 
+        def interleave(c):
+            nc.scalar.copy(
+                out=grouped[c][:].rearrange("p (g i) j -> p g j i", i=PACK),
+                in_=w_raw[c][:].rearrange("p j (g i) -> p g j i", i=PACK),
+            )
+
         def quantize(c):
             nc.vector.quantize_mx(
                 out=w_codes[:, c * P : (c + 1) * P].bitcast(FP8X4),
@@ -65,7 +70,7 @@ def tile_picked_phnorm_none_p_kernel(tc, x_words, x_scales, w1, gamma, res, offs
         pieces = [slice(u * width, (u + 1) * width) for u in range(PIECES)]
         entries = [offsets[:, u * width // 16 : (u + 1) * width // 16] for u in range(PIECES)]
         nc.vector.memset(x_scale[:].bitcast(I32), 0)
-        nc.scalar.copy(out=grouped[0][:], in_=w_raw[0][:].rearrange("p j m -> p m j"))
+        interleave(0)
         nc.vector.tensor_copy(picked_scales[:], scale_table[:].indirect(offsets[:]))
         for i in range(QUADRANT // BLOCK_PARTS):
             queue = nc.scalar if i % 2 == 0 else nc.sync
@@ -83,7 +88,7 @@ def tile_picked_phnorm_none_p_kernel(tc, x_words, x_scales, w1, gamma, res, offs
         with nc.allow_non_contiguous_dma(reason="one value a channel"):
             nc.sync.dma_start(gamma_sb, gamma.rearrange("(c p) o -> p (c o)", p=P))
 
-        nc.scalar.copy(out=grouped[1][:], in_=w_raw[1][:].rearrange("p j m -> p m j"))
+        interleave(1)
 
         accs = [[psum.tile([P, S], F32, name=f"acc{c}_{u}") for u in range(PIECES)] for c in range(tiles)]
         x_codes = keep.tile([P, S], U32, name="x_codes", align_bytes=64)

@@ -111,47 +111,61 @@ def tile_picked_phnorm_none_p_kernel(tc, x_words, x_scales, w1, gamma, res, offs
         unit = 1.0 / (width * width * S)
         h = [keep.tile([P, S + extra], F32, name=f"h{c}") for c in range(tiles)]
         sums = [[keep.tile([P, 1], F32, name=f"sum{c}_{u}") for u in range(PIECES)] for c in range(tiles)]
-        spread = [[keep.tile([P, 1], F32, name=f"spread{c}_{u}") for u in range(PIECES)] for c in range(tiles)]
+        spread = [[keep.tile([P, 1], F32, name=f"spread{c}_{u}", tag=f"spread{c}_{u}") for u in range(PIECES)] for c in range(tiles)]
         squares = keep.tile([P, tiles, S + extra], F32, name="squares")
         base = [keep.tile([P, 1], F32, name=f"base{c}") for c in range(tiles)]
-        mean = [keep.tile([P, 1], F32, name=f"mean{c}") for c in range(tiles)]
+        mean = {}
         rstd = [keep.tile([P, 1], F32, name=f"rstd{c}") for c in range(tiles)]
-        for c in range(tiles):
-            for u, cols in enumerate(pieces):
-                nc.vector.scalar_tensor_tensor(
-                    out=h[c][:, cols], in0=accs[c][u][:, :width], scalar=1.0, in1=res_sb[c][:, cols],
-                    op0=ALU.mult, op1=ALU.add, accum_out=sums[c][u][:],
-                )
-                span = cols if u == 0 else slice(width, S + extra)
-                nc.scalar.activation(
-                    out=squares[:, c, span], in_=h[c][:, span], func=ACT.Square, scale=-float(width),
-                    bias=sums[c][u][:], accum_out=spread[c][u][:],
-                )
-                if u == 0:
-                    nc.gpsimd.tensor_scalar(
-                        out=h[c][:, S:], in0=sums[c][0][:].to_broadcast([P, extra]), scalar1=1.0 / width,
-                        scalar2=0.0, op0=ALU.mult, op1=ALU.add,
-                    )
-                    nc.gpsimd.tensor_scalar(
-                        out=base[c][:], in0=spread[c][0][:], scalar1=unit, scalar2=EPS, op0=ALU.mult, op1=ALU.add,
-                    )
-                else:
-                    nc.vector.tensor_scalar(
-                        out=mean[c][:], in0=sums[c][0][:], scalar1=sums[c][1][:], scalar2=1.0 / S,
-                        op0=ALU.add, op1=ALU.mult,
-                    )
-                    nc.scalar.activation(
-                        out=rstd[c][:], in_=spread[c][1][:], func=ACT.Abs_reciprocal_sqrt, scale=unit, bias=base[c][:],
-                    )
-        for c in range(tiles):
-            centred = keep.tile([P, S], F32, name=f"centred{c}")
-            nc.vector.tensor_scalar(
-                out=centred[:], in0=h[c][:, :S], scalar1=mean[c][:], scalar2=gamma_sb[:, c : c + 1],
-                op0=ALU.subtract, op1=ALU.mult,
+        centred = {}
+
+        def add_and_square(c, u):
+            cols = pieces[u]
+            nc.vector.scalar_tensor_tensor(
+                out=h[c][:, cols], in0=accs[c][u][:, :width], scalar=1.0, in1=res_sb[c][:, cols],
+                op0=ALU.mult, op1=ALU.add, accum_out=sums[c][u][:],
             )
-            for u, cols in enumerate(pieces if c == tiles - 1 else [slice(0, S)]):
+            span = cols if u == 0 else slice(width, S + extra)
+            nc.scalar.activation(
+                out=squares[:, c, span], in_=h[c][:, span], func=ACT.Square, scale=-float(width),
+                bias=sums[c][u][:], accum_out=spread[c][u][:],
+            )
+            if u == 0:
+                nc.gpsimd.tensor_scalar(
+                    out=h[c][:, S:], in0=sums[c][0][:].to_broadcast([P, extra]), scalar1=1.0 / width,
+                    scalar2=0.0, op0=ALU.mult, op1=ALU.add,
+                )
+                nc.gpsimd.tensor_scalar(
+                    out=base[c][:], in0=spread[c][0][:], scalar1=unit, scalar2=EPS, op0=ALU.mult, op1=ALU.add,
+                )
+            else:
+                mean[c] = keep.tile([P, 1], F32, name=f"mean{c}", tag=f"mean{c}")
+                nc.vector.tensor_scalar(
+                    out=mean[c][:], in0=sums[c][0][:], scalar1=sums[c][1][:], scalar2=1.0 / S,
+                    op0=ALU.add, op1=ALU.mult,
+                )
+                nc.scalar.activation(
+                    out=rstd[c][:], in_=spread[c][1][:], func=ACT.Abs_reciprocal_sqrt, scale=unit, bias=base[c][:],
+                )
+
+        def centre(c, parts):
+            centred[c] = keep.tile([P, S], F32, name=f"centred{c}", tag="spread0_1" if c == 1 else "centred0")
+            for cols in parts:
+                nc.vector.tensor_scalar(
+                    out=centred[c][:, cols], in0=h[c][:, cols], scalar1=mean[c][:], scalar2=None, op0=ALU.subtract,
+                )
+
+        def scale_and_store(c, parts):
+            for u, cols in enumerate(parts):
                 result = keep.tile([P, cols.stop - cols.start], F32, name=f"result{c}_{u}")
                 nc.vector.tensor_scalar(
-                    out=result[:], in0=centred[:, cols], scalar1=rstd[c][:], scalar2=None, op0=ALU.mult,
+                    out=result[:], in0=centred[c][:, cols], scalar1=rstd[c][:], scalar2=gamma_sb[:, c : c + 1],
+                    op0=ALU.mult, op1=ALU.mult,
                 )
                 nc.sync.dma_start(out[c * P : (c + 1) * P, cols], result[:])
+
+        for c in range(tiles):
+            for u in range(PIECES):
+                add_and_square(c, u)
+        for c, parts in enumerate([[slice(0, S)], pieces]):
+            centre(c, parts)
+            scale_and_store(c, parts)

@@ -31,14 +31,14 @@ def tile_picked_phnorm_none_p_kernel(tc, x_words, x_scales, w1, gamma, res, offs
         keep = ctx.enter_context(tc.tile_pool(name="keep", bufs=1))
         psum = ctx.enter_context(tc.psum_pool(name="psum", bufs=1))
 
+        reused = ctx.enter_context(tc.tile_pool(name="reused", bufs=1))
         offsets = keep.tile([P, S // 16], U16, name="offsets")
-        nc.sync.dma_start(offsets[:], offs)
-
-        scale_table = keep.tile([P, T], U8, name="scale_table", tag="table_then_res", align_bytes=64)
+        scale_table = reused.tile([P, T], U8, name="scale_table", offset=0, align_bytes=64)
         nc.vector.memset(scale_table[:].bitcast(I32), 0)
         w_rows = w1.rearrange("(p j) m -> p j m", j=PACK)
         w_raw = [keep.tile([P, PACK, P], F32, name=f"w_raw{c}", tag=f"w_raw{c}") for c in range(tiles)]
         nc.sync.dma_start(w_raw[0][:], w_rows[:, :, 0:P])
+        nc.sync.dma_start(offsets[:], offs)
         nc.sync.dma_start(scale_table[0:P:BLOCK_PARTS, :].bitcast(I32), x_scales[0].bitcast(I32))
         word_table = keep.tile([P, T], I32, name="word_table", align_bytes=64)
         nc.sync.dma_start(word_table[:], x_words[0].rearrange("p n t -> p (n t)").bitcast(I32))
@@ -50,7 +50,7 @@ def tile_picked_phnorm_none_p_kernel(tc, x_words, x_scales, w1, gamma, res, offs
 
         grouped = [keep.tile([P, P, PACK], BF16, name=f"grouped{c}", align_bytes=64) for c in range(tiles)]
         w_codes = keep.tile([P, N], U32, name="w_codes", align_bytes=64)
-        w_scale = keep.tile([P, N], U8, name="w_scale", align_bytes=64)
+        w_scale = reused.tile([P, N], U8, name="w_scale", offset=0, align_bytes=64)
 
         def interleave(c):
             nc.scalar.copy(
@@ -79,7 +79,7 @@ def tile_picked_phnorm_none_p_kernel(tc, x_words, x_scales, w1, gamma, res, offs
                 picked_scales[BLOCK_PARTS * i : P : QUADRANT, :].bitcast(I32),
             )
         quantize(0)
-        late = keep.tile([P, tiles * S + tiles], F32, name="late", tag="table_then_res", align_bytes=64)
+        late = reused.tile([P, tiles * S + tiles], F32, name="late", offset=N, align_bytes=64)
         res_sb = [late[:, c * S : (c + 1) * S] for c in range(tiles)]
         for cols in pieces:
             nc.sync.dma_start(res_sb[0][:, cols], res[0:P, cols])
@@ -134,7 +134,8 @@ def tile_picked_phnorm_none_p_kernel(tc, x_words, x_scales, w1, gamma, res, offs
                     out=h[c][:, S:], in0=sums[c][0][:].to_broadcast([P, extra]), scalar1=1.0 / width,
                     scalar2=0.0, op0=ALU.mult, op1=ALU.add,
                 )
-                nc.gpsimd.tensor_scalar(
+                engine = nc.gpsimd if c == 0 else nc.vector
+                engine.tensor_scalar(
                     out=base[c][:], in0=spread[c][0][:], scalar1=unit, scalar2=EPS, op0=ALU.mult, op1=ALU.add,
                 )
             else:

@@ -111,62 +111,48 @@ def tile_picked_phnorm_none_p_kernel(tc, x_words, x_scales, w1, gamma, res, offs
         unit = 1.0 / (width * width * S)
         h = [keep.tile([P, S + extra], F32, name=f"h{c}") for c in range(tiles)]
         sums = [[keep.tile([P, 1], F32, name=f"sum{c}_{u}") for u in range(PIECES)] for c in range(tiles)]
-        spread = [[keep.tile([P, 1], F32, name=f"spread{c}_{u}", tag=f"spread{c}_{u}") for u in range(PIECES)] for c in range(tiles)]
+        spread = [[keep.tile([P, 1], F32, name=f"spread{c}_{u}") for u in range(PIECES)] for c in range(tiles)]
         squares = keep.tile([P, tiles, S + extra], F32, name="squares")
         base = [keep.tile([P, 1], F32, name=f"base{c}") for c in range(tiles)]
-        mean = {}
+        mean = [keep.tile([P, 1], F32, name=f"mean{c}") for c in range(tiles)]
         rstd = [keep.tile([P, 1], F32, name=f"rstd{c}") for c in range(tiles)]
-        centred = {}
-
-        def add_and_square(c, u):
-            cols = pieces[u]
-            nc.vector.scalar_tensor_tensor(
-                out=h[c][:, cols], in0=accs[c][u][:, :width], scalar=1.0, in1=res_sb[c][:, cols],
-                op0=ALU.mult, op1=ALU.add, accum_out=sums[c][u][:],
-            )
-            span = cols if u == 0 else slice(width, S + extra)
-            nc.scalar.activation(
-                out=squares[:, c, span], in_=h[c][:, span], func=ACT.Square, scale=-float(width),
-                bias=sums[c][u][:], accum_out=spread[c][u][:],
-            )
-            if u == 0:
-                nc.gpsimd.tensor_scalar(
-                    out=h[c][:, S:], in0=sums[c][0][:].to_broadcast([P, extra]), scalar1=1.0 / width,
-                    scalar2=0.0, op0=ALU.mult, op1=ALU.add,
+        for c in range(tiles):
+            for u, cols in enumerate(pieces):
+                nc.vector.scalar_tensor_tensor(
+                    out=h[c][:, cols], in0=accs[c][u][:, :width], scalar=1.0, in1=res_sb[c][:, cols],
+                    op0=ALU.mult, op1=ALU.add, accum_out=sums[c][u][:],
                 )
-                engine = nc.gpsimd if c == 0 else nc.vector
-                engine.tensor_scalar(
-                    out=base[c][:], in0=spread[c][0][:], scalar1=unit, scalar2=EPS, op0=ALU.mult, op1=ALU.add,
-                )
-            else:
-                mean[c] = keep.tile([P, 1], F32, name=f"mean{c}", tag=f"mean{c}")
-                nc.vector.tensor_scalar(
-                    out=mean[c][:], in0=sums[c][0][:], scalar1=sums[c][1][:], scalar2=1.0 / S,
-                    op0=ALU.add, op1=ALU.mult,
-                )
+                span = cols if u == 0 else slice(width, S + extra)
                 nc.scalar.activation(
-                    out=rstd[c][:], in_=spread[c][1][:], func=ACT.Abs_reciprocal_sqrt, scale=unit, bias=base[c][:],
+                    out=squares[:, c, span], in_=h[c][:, span], func=ACT.Square, scale=-float(width),
+                    bias=sums[c][u][:], accum_out=spread[c][u][:],
                 )
-
-        def centre(c, parts):
-            centred[c] = keep.tile([P, S], F32, name=f"centred{c}", tag="spread0_1" if c == 1 else "centred0")
-            for cols in parts:
-                nc.vector.tensor_scalar(
-                    out=centred[c][:, cols], in0=h[c][:, cols], scalar1=mean[c][:], scalar2=None, op0=ALU.subtract,
-                )
-
-        def scale_and_store(c, parts):
-            for u, cols in enumerate(parts):
+                if u == 0:
+                    nc.gpsimd.tensor_scalar(
+                        out=h[c][:, S:], in0=sums[c][0][:].to_broadcast([P, extra]), scalar1=1.0 / width,
+                        scalar2=0.0, op0=ALU.mult, op1=ALU.add,
+                    )
+                    engine = nc.gpsimd if c == 0 else nc.vector
+                    engine.tensor_scalar(
+                        out=base[c][:], in0=spread[c][0][:], scalar1=unit, scalar2=EPS, op0=ALU.mult, op1=ALU.add,
+                    )
+                else:
+                    nc.vector.tensor_scalar(
+                        out=mean[c][:], in0=sums[c][0][:], scalar1=sums[c][1][:], scalar2=1.0 / S,
+                        op0=ALU.add, op1=ALU.mult,
+                    )
+                    nc.scalar.activation(
+                        out=rstd[c][:], in_=spread[c][1][:], func=ACT.Abs_reciprocal_sqrt, scale=unit, bias=base[c][:],
+                    )
+        for c in range(tiles):
+            centred = keep.tile([P, S], F32, name=f"centred{c}")
+            nc.vector.tensor_scalar(
+                out=centred[:], in0=h[c][:, :S], scalar1=mean[c][:], scalar2=gamma_sb[:, c : c + 1],
+                op0=ALU.subtract, op1=ALU.mult,
+            )
+            for u, cols in enumerate(pieces if c == tiles - 1 else [slice(0, S)]):
                 result = keep.tile([P, cols.stop - cols.start], F32, name=f"result{c}_{u}")
                 nc.vector.tensor_scalar(
-                    out=result[:], in0=centred[c][:, cols], scalar1=rstd[c][:], scalar2=gamma_sb[:, c : c + 1],
-                    op0=ALU.mult, op1=ALU.mult,
+                    out=result[:], in0=centred[:, cols], scalar1=rstd[c][:], scalar2=None, op0=ALU.mult,
                 )
                 nc.sync.dma_start(out[c * P : (c + 1) * P, cols], result[:])
-
-        for c in range(tiles):
-            for u in range(PIECES):
-                add_and_square(c, u)
-        for c, parts in enumerate([[slice(0, S)], pieces]):
-            centre(c, parts)
-            scale_and_store(c, parts)

@@ -114,7 +114,7 @@ def tile_picked_phnorm_none_p_kernel(tc, x_words, x_scales, w1, gamma, res, offs
         spread = [[keep.tile([P, 1], F32, name=f"spread{c}_{u}") for u in range(PIECES)] for c in range(tiles)]
         squares = keep.tile([P, tiles, S + extra], F32, name="squares")
         base = [keep.tile([P, 1], F32, name=f"base{c}") for c in range(tiles)]
-        mean = [keep.tile([P, 1], F32, name=f"mean{c}") for c in range(tiles)]
+        mean = [res_sb[1][:, 0:1], keep.tile([P, 1], F32, name="last_mean")[:]]
         rstd = [keep.tile([P, 1], F32, name=f"rstd{c}") for c in range(tiles)]
         for c in range(tiles):
             for u, cols in enumerate(pieces):
@@ -137,17 +137,17 @@ def tile_picked_phnorm_none_p_kernel(tc, x_words, x_scales, w1, gamma, res, offs
                         out=base[c][:], in0=spread[c][0][:], scalar1=unit, scalar2=EPS, op0=ALU.mult, op1=ALU.add,
                     )
                 else:
-                    nc.vector.tensor_scalar(
-                        out=mean[c][:], in0=sums[c][0][:], scalar1=sums[c][1][:], scalar2=1.0 / S,
-                        op0=ALU.add, op1=ALU.mult,
-                    )
                     nc.scalar.activation(
                         out=rstd[c][:], in_=spread[c][1][:], func=ACT.Abs_reciprocal_sqrt, scale=unit, bias=base[c][:],
                     )
         for c in range(tiles):
+            nc.vector.tensor_scalar(
+                out=mean[c], in0=sums[c][0][:], scalar1=sums[c][1][:], scalar2=1.0 / S, op0=ALU.add, op1=ALU.mult,
+            )
+        for c in range(tiles):
             centred = keep.tile([P, S], F32, name=f"centred{c}")
             nc.vector.tensor_scalar(
-                out=centred[:], in0=h[c][:, :S], scalar1=mean[c][:], scalar2=gamma_sb[:, c : c + 1],
+                out=centred[:], in0=h[c][:, :S], scalar1=mean[c], scalar2=gamma_sb[:, c : c + 1],
                 op0=ALU.subtract, op1=ALU.mult,
             )
             for u, cols in enumerate(pieces if c == tiles - 1 else [slice(0, S)]):

@@ -20,27 +20,30 @@ PACK = 4
 BLOCK_PARTS = 8
 QUADRANT = 32
 EPS = 1e-5
-PIECES = 2
+HALF = S // 2
+TERMS = 4
+GAIN = 2.0 * S
 
 
 def tile_picked_phnorm_none_p_kernel(tc, x_words, x_scales, w1, gamma, res, offs, out):
     nc = tc.nc
     tiles = N // P
-    width = S // PIECES
+    halves = [slice(0, HALF), slice(HALF, S)]
     with ExitStack() as ctx:
         keep = ctx.enter_context(tc.tile_pool(name="keep", bufs=1))
+        placed = ctx.enter_context(tc.tile_pool(name="placed", bufs=1))
         psum = ctx.enter_context(tc.psum_pool(name="psum", bufs=1))
 
-        reused = ctx.enter_context(tc.tile_pool(name="reused", bufs=1))
         offsets = keep.tile([P, S // 16], U16, name="offsets")
-        scale_table = reused.tile([P, T], U8, name="scale_table", offset=0, align_bytes=64)
+        scale_table = placed.tile([P, T], U8, name="scale_table", offset=0, align_bytes=64)
         nc.vector.memset(scale_table[:].bitcast(I32), 0)
+
         w_rows = w1.rearrange("(p j) m -> p j m", j=PACK)
-        w_raw = [keep.tile([P, PACK, P], F32, name=f"w_raw{c}", tag=f"w_raw{c}") for c in range(tiles)]
+        w_raw = [keep.tile([P, PACK, P], F32, name=f"w_raw{c}") for c in range(tiles)]
+        word_table = keep.tile([P, T], I32, name="word_table", align_bytes=64)
         nc.sync.dma_start(w_raw[0][:], w_rows[:, :, 0:P])
         nc.sync.dma_start(offsets[:], offs)
         nc.sync.dma_start(scale_table[0:P:BLOCK_PARTS, :].bitcast(I32), x_scales[0].bitcast(I32))
-        word_table = keep.tile([P, T], I32, name="word_table", align_bytes=64)
         nc.sync.dma_start(word_table[:], x_words[0].rearrange("p n t -> p (n t)").bitcast(I32))
         nc.sync.dma_start(w_raw[1][:], w_rows[:, :, P : 2 * P])
 
@@ -48,9 +51,18 @@ def tile_picked_phnorm_none_p_kernel(tc, x_words, x_scales, w1, gamma, res, offs
         nc.vector.memset(warm[:, 0:1], 1.0)
         nc.scalar.activation(out=warm[:, 1:2], in_=warm[:, 0:1], func=ACT.Abs_reciprocal_sqrt)
 
+        res_bytes = HALF * 4
+        w_scale = placed.tile([P, N], U8, name="w_scale", offset=0, align_bytes=64)
+        gamma_sb = placed.tile([P, tiles], F32, name="gamma_sb", offset=N, align_bytes=64)
+        res_at = N + 64
+        res_first = placed.tile([P, HALF], F32, name="res_first", offset=res_at, align_bytes=64)
+        res_rest = placed.tile([P, HALF + S], F32, name="res_rest", offset=res_at + res_bytes, align_bytes=64)
+        res_sb = [[res_first[:], res_rest[:, :HALF]], [res_rest[:, HALF:S], res_rest[:, S:]]]
         grouped = [keep.tile([P, P, PACK], BF16, name=f"grouped{c}", align_bytes=64) for c in range(tiles)]
-        w_codes = keep.tile([P, N], U32, name="w_codes", align_bytes=64)
-        w_scale = reused.tile([P, N], U8, name="w_scale", offset=0, align_bytes=64)
+        w_codes = [
+            keep.tile([P, P], U32, name="w_codes0", align_bytes=64),
+            keep.tile([P, P], U32, name="w_codes1", align_bytes=64),
+        ]
 
         def interleave(c):
             nc.scalar.copy(
@@ -60,15 +72,13 @@ def tile_picked_phnorm_none_p_kernel(tc, x_words, x_scales, w1, gamma, res, offs
 
         def quantize(c):
             nc.vector.quantize_mx(
-                out=w_codes[:, c * P : (c + 1) * P].bitcast(FP8X4),
+                out=w_codes[c][:].bitcast(FP8X4),
                 scales=w_scale[:, c * P : (c + 1) * P],
                 in_=grouped[c][:].rearrange("p m j -> p (m j)"),
             )
 
         x_scale = keep.tile([P, S], U8, name="x_scale", align_bytes=64)
         picked_scales = keep.tile([P, S], U8, name="picked_scales", align_bytes=64)
-        pieces = [slice(u * width, (u + 1) * width) for u in range(PIECES)]
-        entries = [offsets[:, u * width // 16 : (u + 1) * width // 16] for u in range(PIECES)]
         nc.vector.memset(x_scale[:].bitcast(I32), 0)
         interleave(0)
         nc.vector.tensor_copy(picked_scales[:], scale_table[:].indirect(offsets[:]))
@@ -79,27 +89,47 @@ def tile_picked_phnorm_none_p_kernel(tc, x_words, x_scales, w1, gamma, res, offs
                 picked_scales[BLOCK_PARTS * i : P : QUADRANT, :].bitcast(I32),
             )
         quantize(0)
-        late = reused.tile([P, tiles * S + tiles], F32, name="late", offset=N, align_bytes=64)
-        res_sb = [late[:, c * S : (c + 1) * S] for c in range(tiles)]
-        for cols in pieces:
-            nc.sync.dma_start(res_sb[0][:, cols], res[0:P, cols])
-        nc.sync.dma_start(res_sb[1], res[P : 2 * P, :])
-        gamma_sb = late[:, tiles * S :]
+        for u, cols in enumerate(halves):
+            nc.sync.dma_start(res_sb[0][u], res[0:P, cols])
+        nc.sync.dma_start(res_rest[:, HALF:], res[P : 2 * P, :])
         with nc.allow_non_contiguous_dma(reason="one value a channel"):
-            nc.sync.dma_start(gamma_sb, gamma.rearrange("(c p) o -> p (c o)", p=P))
-
+            nc.sync.dma_start(gamma_sb[:], gamma.rearrange("(c p) o -> p (c o)", p=P))
         interleave(1)
 
-        accs = [[psum.tile([P, S], F32, name=f"acc{c}_{u}") for u in range(PIECES)] for c in range(tiles)]
         x_codes = keep.tile([P, S], U32, name="x_codes", align_bytes=64)
-        for u, cols in enumerate(pieces):
-            nc.vector.tensor_copy(x_codes[:, cols], word_table[:].bitcast(U32).indirect(entries[u]))
-        quantize(1)
-        for c in range(tiles):
-            for u, cols in enumerate(pieces):
+        for cols in halves:
+            entries = offsets[:, cols.start // 16 : cols.stop // 16]
+            nc.vector.tensor_copy(x_codes[:, cols], word_table[:].bitcast(U32).indirect(entries))
+
+        accs = [[psum.tile([P, S], F32, name=f"acc{c}_{u}") for u in range(2)] for c in range(tiles)]
+        h = [keep.tile([P, S], F32, name=f"h{c}") for c in range(tiles)]
+        gained = [keep.tile([P, S], F32, name=f"gained{c}") for c in range(tiles)]
+        squares = keep.tile([P, tiles, S + TERMS], F32, name="squares")
+
+        def column(name):
+            return keep.tile([P, 1], F32, name=name)[:]
+
+        sums = [keep.tile([P, 2], F32, name=f"sums{c}") for c in range(tiles)]
+        terms = keep.tile([P, tiles, TERMS], F32, name="terms")
+        second = [column(f"second{c}") for c in range(tiles)]
+        distance = [column(f"distance{c}") for c in range(tiles)]
+        base = [column(f"base{c}") for c in range(tiles)]
+        shift = [column(f"shift{c}") for c in range(tiles)]
+        rstd = [column(f"rstd{c}") for c in range(tiles)]
+        weighted = keep.tile([P, tiles, 2], F32, name="weighted")
+        factor = keep.tile([P, 2], F32, name="factor")
+        unit = GAIN * GAIN / (HALF * HALF * S)
+        nc.vector.memset(factor[:], GAIN / S)
+        nc.vector.memset(terms[:, :, 2:], 0.0)
+        nc.vector.tensor_scalar(
+            out=terms[:, :, 1], in0=factor[:], scalar1=EPS * GAIN * S / unit, scalar2=None, op0=ALU.mult,
+        )
+
+        def multiply(c):
+            for u, cols in enumerate(halves):
                 nc.tensor.matmul_mx(
-                    out=accs[c][u][:, :width],
-                    lhsT=w_codes[:, c * P : (c + 1) * P].bitcast(FP8X4),
+                    out=accs[c][u][:, :HALF],
+                    lhsT=w_codes[c][:].bitcast(FP8X4),
                     lhsT_scale=w_scale[:, c * P : (c + 1) * P],
                     rhs=x_codes[:, cols].bitcast(FP8X4),
                     rhs_scale=x_scale[:, cols],
@@ -107,52 +137,61 @@ def tile_picked_phnorm_none_p_kernel(tc, x_words, x_scales, w1, gamma, res, offs
                     stop=True,
                 )
 
-        extra = width // 2
-        unit = 1.0 / (width * width * S)
-        h = [keep.tile([P, S + extra], F32, name=f"h{c}") for c in range(tiles)]
-        sums = [[keep.tile([P, 1], F32, name=f"sum{c}_{u}") for u in range(PIECES)] for c in range(tiles)]
-        spread = [[keep.tile([P, 1], F32, name=f"spread{c}_{u}") for u in range(PIECES)] for c in range(tiles)]
-        squares = keep.tile([P, tiles, S + extra], F32, name="squares")
-        base = [keep.tile([P, 1], F32, name=f"base{c}") for c in range(tiles)]
-        mean = [res_sb[1][:, 0:1], keep.tile([P, 1], F32, name="last_mean")[:]]
-        rstd = [keep.tile([P, 1], F32, name=f"rstd{c}") for c in range(tiles)]
-        for c in range(tiles):
-            for u, cols in enumerate(pieces):
-                nc.vector.scalar_tensor_tensor(
-                    out=h[c][:, cols], in0=accs[c][u][:, :width], scalar=1.0, in1=res_sb[c][:, cols],
-                    op0=ALU.mult, op1=ALU.add, accum_out=sums[c][u][:],
-                )
-                span = cols if u == 0 else slice(width, S + extra)
-                nc.scalar.activation(
-                    out=squares[:, c, span], in_=h[c][:, span], func=ACT.Square, scale=-float(width),
-                    bias=sums[c][u][:], accum_out=spread[c][u][:],
-                )
-                if u == 0:
-                    nc.gpsimd.tensor_scalar(
-                        out=h[c][:, S:], in0=sums[c][0][:].to_broadcast([P, extra]), scalar1=1.0 / width,
-                        scalar2=0.0, op0=ALU.mult, op1=ALU.add,
-                    )
-                    engine = nc.gpsimd if c == 0 else nc.vector
-                    engine.tensor_scalar(
-                        out=base[c][:], in0=spread[c][0][:], scalar1=unit, scalar2=EPS, op0=ALU.mult, op1=ALU.add,
-                    )
-                else:
-                    nc.scalar.activation(
-                        out=rstd[c][:], in_=spread[c][1][:], func=ACT.Abs_reciprocal_sqrt, scale=unit, bias=base[c][:],
-                    )
-        for c in range(tiles):
-            nc.vector.tensor_scalar(
-                out=mean[c], in0=sums[c][0][:], scalar1=sums[c][1][:], scalar2=1.0 / S, op0=ALU.add, op1=ALU.mult,
+        def add(c, u):
+            nc.vector.scalar_tensor_tensor(
+                out=h[c][:, halves[u]], in0=accs[c][u][:, :HALF], scalar=1.0, in1=res_sb[c][u],
+                op0=ALU.mult, op1=ALU.add, accum_out=sums[c][:, u : u + 1],
             )
-        for c in range(tiles):
-            centred = keep.tile([P, S], F32, name=f"centred{c}")
+
+        def square(c, u):
+            nc.scalar.activation(
+                out=squares[:, c, halves[u]], in_=h[c][:, halves[u]], func=ACT.Square, scale=-float(HALF),
+                bias=sums[c][:, u : u + 1], accum_out=terms[:, c, 0:1] if u == 0 else second[c],
+            )
+
+        def inverse_root(c):
+            nc.scalar.activation(
+                out=squares[:, c, S:], in_=terms[:, c, :], func=ACT.Identity, scale=unit, bias=distance[c],
+                accum_out=base[c],
+            )
+            nc.scalar.activation(out=rstd[c], in_=second[c], func=ACT.Abs_reciprocal_sqrt, scale=unit, bias=base[c])
+
+        def gain(c):
             nc.vector.tensor_scalar(
-                out=centred[:], in0=h[c][:, :S], scalar1=mean[c], scalar2=gamma_sb[:, c : c + 1],
+                out=gained[c][:], in0=h[c][:], scalar1=gamma_sb[:, c : c + 1], scalar2=GAIN,
+                op0=ALU.mult, op1=ALU.mult,
+            )
+
+        def shifted_mean(c):
+            nc.vector.scalar_tensor_tensor(
+                out=weighted[:, c, :], in0=sums[c][:], scalar=gamma_sb[:, c : c + 1], in1=factor[:],
+                op0=ALU.mult, op1=ALU.mult, accum_out=shift[c],
+            )
+
+        def finish(c, cols):
+            result = keep.tile([P, cols.stop - cols.start], F32, name=f"result{c}_{cols.start}")
+            nc.vector.tensor_scalar(
+                out=result[:], in0=gained[c][:, cols], scalar1=shift[c], scalar2=rstd[c],
                 op0=ALU.subtract, op1=ALU.mult,
             )
-            for u, cols in enumerate(pieces if c == tiles - 1 else [slice(0, S)]):
-                result = keep.tile([P, cols.stop - cols.start], F32, name=f"result{c}_{u}")
-                nc.vector.tensor_scalar(
-                    out=result[:], in0=centred[:, cols], scalar1=rstd[c][:], scalar2=None, op0=ALU.mult,
-                )
-                nc.sync.dma_start(out[c * P : (c + 1) * P, cols], result[:])
+            nc.sync.dma_start(out[c * P : (c + 1) * P, cols], result[:])
+
+        quantize(1)
+        for c in range(tiles):
+            multiply(c)
+        for c in range(tiles):
+            add(c, 0)
+            square(c, 0)
+            add(c, 1)
+            nc.scalar.activation(
+                out=distance[c], in_=sums[c][:, 1:2], func=ACT.Square, scale=-1.0, bias=sums[c][:, 0:1],
+            )
+            square(c, 1)
+            inverse_root(c)
+        gain(0)
+        shifted_mean(0)
+        shifted_mean(1)
+        finish(0, slice(0, S))
+        gain(1)
+        for cols in halves:
+            finish(1, cols)

@@ -22,6 +22,7 @@ QUADRANT = 32
 EPS = 1e-5
 HALF = S // 2
 TERMS = 4
+LAP = 8
 GAIN = 2.0 * S
 
 
@@ -43,8 +44,13 @@ def tile_picked_phnorm_none_p_kernel(tc, x_words, x_scales, w1, gamma, res, offs
         word_table = keep.tile([P, T], I32, name="word_table", align_bytes=64)
         nc.sync.dma_start(w_raw[0][:], w_rows[:, :, 0:P])
         nc.sync.dma_start(offsets[:], offs)
+        gamma_rows = keep.tile([P, QUADRANT], F32, name="gamma_rows", align_bytes=64)
+        nc.vector.memset(gamma_rows[:], 0.0)
         nc.sync.dma_start(scale_table[0:P:BLOCK_PARTS, :].bitcast(I32), x_scales[0].bitcast(I32))
         nc.sync.dma_start(word_table[:], x_words[0].rearrange("p n t -> p (n t)").bitcast(I32))
+        nc.sync.dma_start(
+            gamma_rows[0 : P : QUADRANT // tiles, :], gamma.rearrange("(c q i) o -> q c (i o)", c=tiles, i=QUADRANT),
+        )
         nc.sync.dma_start(w_raw[1][:], w_rows[:, :, P : 2 * P])
 
         warm = keep.tile([P, 2], F32, name="warm")
@@ -53,11 +59,12 @@ def tile_picked_phnorm_none_p_kernel(tc, x_words, x_scales, w1, gamma, res, offs
 
         res_bytes = HALF * 4
         w_scale = placed.tile([P, N], U8, name="w_scale", offset=0, align_bytes=64)
-        gamma_sb = placed.tile([P, tiles], F32, name="gamma_sb", offset=N, align_bytes=64)
-        res_at = N + 64
+        gamma_cols = placed.tile([P, QUADRANT], F32, name="gamma_cols", offset=N, align_bytes=64)
+        gamma_sb = keep.tile([P, tiles], F32, name="gamma_sb")
+        res_at = N + QUADRANT * 4
         res_first = placed.tile([P, HALF], F32, name="res_first", offset=res_at, align_bytes=64)
-        res_rest = placed.tile([P, HALF + S], F32, name="res_rest", offset=res_at + res_bytes, align_bytes=64)
-        res_sb = [[res_first[:], res_rest[:, :HALF]], [res_rest[:, HALF:S], res_rest[:, S:]]]
+        res_rest = placed.tile([P, 2 * S], F32, name="res_rest", offset=res_at + res_bytes, align_bytes=64)
+        res_sb = [[res_first[:], res_rest[:, HALF:S]], [res_rest[:, S : S + HALF], res_rest[:, S + HALF :]]]
         grouped = [keep.tile([P, P, PACK], BF16, name=f"grouped{c}", align_bytes=64) for c in range(tiles)]
         w_codes = [
             keep.tile([P, P], U32, name="w_codes0", align_bytes=64),
@@ -89,11 +96,14 @@ def tile_picked_phnorm_none_p_kernel(tc, x_words, x_scales, w1, gamma, res, offs
                 picked_scales[BLOCK_PARTS * i : P : QUADRANT, :].bitcast(I32),
             )
         quantize(0)
+        nc.vector.transpose(gamma_cols[:], gamma_rows[:])
+        nc.vector.tensor_scalar(
+            out=gamma_sb[:], in0=gamma_cols[:, 0 : QUADRANT : QUADRANT // tiles], scalar1=GAIN / S, scalar2=None,
+            op0=ALU.mult,
+        )
         for u, cols in enumerate(halves):
             nc.sync.dma_start(res_sb[0][u], res[0:P, cols])
-        nc.sync.dma_start(res_rest[:, HALF:], res[P : 2 * P, :])
-        with nc.allow_non_contiguous_dma(reason="one value a channel"):
-            nc.sync.dma_start(gamma_sb[:], gamma.rearrange("(c p) o -> p (c o)", p=P))
+        nc.sync.dma_start(res_rest[:, S:], res[P : 2 * P, :])
         interleave(1)
 
         x_codes = keep.tile([P, S], U32, name="x_codes", align_bytes=64)
@@ -103,7 +113,7 @@ def tile_picked_phnorm_none_p_kernel(tc, x_words, x_scales, w1, gamma, res, offs
 
         accs = [[psum.tile([P, S], F32, name=f"acc{c}_{u}") for u in range(2)] for c in range(tiles)]
         h = [keep.tile([P, S], F32, name=f"h{c}") for c in range(tiles)]
-        gained = [keep.tile([P, S], F32, name=f"gained{c}") for c in range(tiles)]
+        gained = [res_rest[:, LAP : S + LAP], keep.tile([P, S], F32, name="gained1")[:]]
         squares = keep.tile([P, tiles, S + TERMS], F32, name="squares")
 
         def column(name):
@@ -112,17 +122,16 @@ def tile_picked_phnorm_none_p_kernel(tc, x_words, x_scales, w1, gamma, res, offs
         sums = [keep.tile([P, 2], F32, name=f"sums{c}") for c in range(tiles)]
         terms = keep.tile([P, tiles, TERMS], F32, name="terms")
         second = [column(f"second{c}") for c in range(tiles)]
-        distance = [column(f"distance{c}") for c in range(tiles)]
+        distance = [squares[:, 1, 0:1], column("distance1")]
         base = [column(f"base{c}") for c in range(tiles)]
-        shift = [column(f"shift{c}") for c in range(tiles)]
+        shift = [res_rest[:, S + LAP : S + LAP + 1], column("shift1")]
         rstd = [column(f"rstd{c}") for c in range(tiles)]
-        weighted = keep.tile([P, tiles, 2], F32, name="weighted")
-        factor = keep.tile([P, 2], F32, name="factor")
+        ones = keep.tile([P, tiles], F32, name="ones")
         unit = GAIN * GAIN / (HALF * HALF * S)
-        nc.vector.memset(factor[:], GAIN / S)
+        nc.vector.memset(ones[:], 1.0)
         nc.vector.memset(terms[:, :, 2:], 0.0)
         nc.vector.tensor_scalar(
-            out=terms[:, :, 1], in0=factor[:], scalar1=EPS * GAIN * S / unit, scalar2=None, op0=ALU.mult,
+            out=terms[:, :, 1], in0=ones[:], scalar1=EPS * GAIN * GAIN / unit, scalar2=None, op0=ALU.mult,
         )
 
         def multiply(c):
@@ -156,16 +165,16 @@ def tile_picked_phnorm_none_p_kernel(tc, x_words, x_scales, w1, gamma, res, offs
             )
             nc.scalar.activation(out=rstd[c], in_=second[c], func=ACT.Abs_reciprocal_sqrt, scale=unit, bias=base[c])
 
-        def gain(c):
+        def gain(c, cols):
             nc.vector.tensor_scalar(
-                out=gained[c][:], in0=h[c][:], scalar1=gamma_sb[:, c : c + 1], scalar2=GAIN,
+                out=gained[c][:, cols], in0=h[c][:, cols], scalar1=gamma_sb[:, c : c + 1], scalar2=float(S),
                 op0=ALU.mult, op1=ALU.mult,
             )
 
         def shifted_mean(c):
-            nc.vector.scalar_tensor_tensor(
-                out=weighted[:, c, :], in0=sums[c][:], scalar=gamma_sb[:, c : c + 1], in1=factor[:],
-                op0=ALU.mult, op1=ALU.mult, accum_out=shift[c],
+            nc.vector.tensor_scalar(
+                out=shift[c], in0=sums[c][:, 0:1], scalar1=sums[c][:, 1:2], scalar2=gamma_sb[:, c : c + 1],
+                op0=ALU.add, op1=ALU.mult,
             )
 
         def finish(c, cols):
@@ -188,10 +197,11 @@ def tile_picked_phnorm_none_p_kernel(tc, x_words, x_scales, w1, gamma, res, offs
             )
             square(c, 1)
             inverse_root(c)
-        gain(0)
         shifted_mean(0)
-        shifted_mean(1)
+        gain(0, slice(0, S))
         finish(0, slice(0, S))
-        gain(1)
+        shifted_mean(1)
+        for cols in halves:
+            gain(1, cols)
         for cols in halves:
             finish(1, cols)

@@ -59,9 +59,9 @@ def tile_picked_phnorm_none_p_kernel(tc, x_words, x_scales, w1, gamma, res, offs
 
         res_bytes = HALF * 4
         w_scale = placed.tile([P, N], U8, name="w_scale", offset=0, align_bytes=64)
-        gamma_cols = placed.tile([P, QUADRANT], F32, name="gamma_cols", offset=N, align_bytes=64)
-        gamma_sb = keep.tile([P, tiles], F32, name="gamma_sb")
-        res_at = N + QUADRANT * 4
+        gamma_cols = keep.tile([P, QUADRANT], F32, name="gamma_cols", align_bytes=64)
+        gamma_sb = gamma_cols[:, 0 : QUADRANT : QUADRANT // tiles]
+        res_at = N
         res_first = placed.tile([P, HALF], F32, name="res_first", offset=res_at, align_bytes=64)
         res_rest = placed.tile([P, 2 * S], F32, name="res_rest", offset=res_at + res_bytes, align_bytes=64)
         res_sb = [[res_first[:], res_rest[:, HALF:S]], [res_rest[:, S : S + HALF], res_rest[:, S + HALF :]]]
@@ -96,11 +96,6 @@ def tile_picked_phnorm_none_p_kernel(tc, x_words, x_scales, w1, gamma, res, offs
                 picked_scales[BLOCK_PARTS * i : P : QUADRANT, :].bitcast(I32),
             )
         quantize(0)
-        nc.vector.transpose(gamma_cols[:], gamma_rows[:])
-        nc.vector.tensor_scalar(
-            out=gamma_sb[:], in0=gamma_cols[:, 0 : QUADRANT : QUADRANT // tiles], scalar1=GAIN / S, scalar2=None,
-            op0=ALU.mult,
-        )
         for u, cols in enumerate(halves):
             nc.sync.dma_start(res_sb[0][u], res[0:P, cols])
         nc.sync.dma_start(res_rest[:, S:], res[P : 2 * P, :])
@@ -110,6 +105,8 @@ def tile_picked_phnorm_none_p_kernel(tc, x_words, x_scales, w1, gamma, res, offs
         for cols in halves:
             entries = offsets[:, cols.start // 16 : cols.stop // 16]
             nc.vector.tensor_copy(x_codes[:, cols], word_table[:].bitcast(U32).indirect(entries))
+
+        nc.vector.transpose(gamma_cols[:], gamma_rows[:])
 
         accs = [[psum.tile([P, S], F32, name=f"acc{c}_{u}") for u in range(2)] for c in range(tiles)]
         h = [keep.tile([P, S], F32, name=f"h{c}") for c in range(tiles)]
@@ -126,6 +123,7 @@ def tile_picked_phnorm_none_p_kernel(tc, x_words, x_scales, w1, gamma, res, offs
         base = [column(f"base{c}") for c in range(tiles)]
         shift = [res_rest[:, S + LAP : S + LAP + 1], column("shift1")]
         rstd = [column(f"rstd{c}") for c in range(tiles)]
+        weighted = keep.tile([P, tiles, 2, 2], F32, name="weighted")
         ones = keep.tile([P, tiles], F32, name="ones")
         unit = GAIN * GAIN / (HALF * HALF * S)
         nc.vector.memset(ones[:], 1.0)
@@ -167,14 +165,14 @@ def tile_picked_phnorm_none_p_kernel(tc, x_words, x_scales, w1, gamma, res, offs
 
         def gain(c, cols):
             nc.vector.tensor_scalar(
-                out=gained[c][:, cols], in0=h[c][:, cols], scalar1=gamma_sb[:, c : c + 1], scalar2=float(S),
+                out=gained[c][:, cols], in0=h[c][:, cols], scalar1=gamma_sb[:, c : c + 1], scalar2=GAIN,
                 op0=ALU.mult, op1=ALU.mult,
             )
 
         def shifted_mean(c):
             nc.vector.tensor_scalar(
-                out=shift[c], in0=sums[c][:, 0:1], scalar1=sums[c][:, 1:2], scalar2=gamma_sb[:, c : c + 1],
-                op0=ALU.add, op1=ALU.mult,
+                out=weighted[:, c], in0=sums[c][:].unsqueeze(1).to_broadcast([P, 2, 2]),
+                scalar1=gamma_sb[:, c : c + 1], scalar2=None, op0=ALU.mult, op1=ALU.add, accum_out=shift[c],
             )
 
         def finish(c, cols):

@@ -44,13 +44,8 @@ def tile_picked_phnorm_none_p_kernel(tc, x_words, x_scales, w1, gamma, res, offs
         word_table = keep.tile([P, T], I32, name="word_table", align_bytes=64)
         nc.sync.dma_start(w_raw[0][:], w_rows[:, :, 0:P])
         nc.sync.dma_start(offsets[:], offs)
-        gamma_rows = keep.tile([P, QUADRANT], F32, name="gamma_rows", align_bytes=64)
-        nc.vector.memset(gamma_rows[:], 0.0)
         nc.sync.dma_start(scale_table[0:P:BLOCK_PARTS, :].bitcast(I32), x_scales[0].bitcast(I32))
         nc.sync.dma_start(word_table[:], x_words[0].rearrange("p n t -> p (n t)").bitcast(I32))
-        nc.sync.dma_start(
-            gamma_rows[0 : P : QUADRANT // tiles, :], gamma.rearrange("(c q i) o -> q c (i o)", c=tiles, i=QUADRANT),
-        )
         nc.sync.dma_start(w_raw[1][:], w_rows[:, :, P : 2 * P])
 
         warm = keep.tile([P, 2], F32, name="warm")
@@ -59,9 +54,8 @@ def tile_picked_phnorm_none_p_kernel(tc, x_words, x_scales, w1, gamma, res, offs
 
         res_bytes = HALF * 4
         w_scale = placed.tile([P, N], U8, name="w_scale", offset=0, align_bytes=64)
-        gamma_cols = keep.tile([P, QUADRANT], F32, name="gamma_cols", align_bytes=64)
-        gamma_sb = gamma_cols[:, 0 : QUADRANT : QUADRANT // tiles]
-        res_at = N
+        gamma_sb = placed.tile([P, tiles], F32, name="gamma_sb", offset=N, align_bytes=64)
+        res_at = N + 64
         res_first = placed.tile([P, HALF], F32, name="res_first", offset=res_at, align_bytes=64)
         res_rest = placed.tile([P, 2 * S], F32, name="res_rest", offset=res_at + res_bytes, align_bytes=64)
         res_sb = [[res_first[:], res_rest[:, HALF:S]], [res_rest[:, S : S + HALF], res_rest[:, S + HALF :]]]
@@ -99,14 +93,14 @@ def tile_picked_phnorm_none_p_kernel(tc, x_words, x_scales, w1, gamma, res, offs
         for u, cols in enumerate(halves):
             nc.sync.dma_start(res_sb[0][u], res[0:P, cols])
         nc.sync.dma_start(res_rest[:, S:], res[P : 2 * P, :])
+        with nc.allow_non_contiguous_dma(reason="one value a channel"):
+            nc.sync.dma_start(gamma_sb[:], gamma.rearrange("(c p) o -> p (c o)", p=P))
         interleave(1)
 
         x_codes = keep.tile([P, S], U32, name="x_codes", align_bytes=64)
         for cols in halves:
             entries = offsets[:, cols.start // 16 : cols.stop // 16]
             nc.vector.tensor_copy(x_codes[:, cols], word_table[:].bitcast(U32).indirect(entries))
-
-        nc.vector.transpose(gamma_cols[:], gamma_rows[:])
 
         accs = [[psum.tile([P, S], F32, name=f"acc{c}_{u}") for u in range(2)] for c in range(tiles)]
         h = [keep.tile([P, S], F32, name=f"h{c}") for c in range(tiles)]

@@ -115,7 +115,7 @@ def tile_picked_phnorm_none_p_kernel(tc, x_words, x_scales, w1, gamma, res, offs
         second = [column(f"second{c}") for c in range(tiles)]
         distance = [squares[:, 1, 0:1], column("distance1")]
         base = [column(f"base{c}") for c in range(tiles)]
-        shift = [res_rest[:, S + LAP : S + LAP + 1], column("shift1")]
+        shift = [column(f"shift{c}") for c in range(tiles)]
         rstd = [column(f"rstd{c}") for c in range(tiles)]
         weighted = keep.tile([P, tiles, 2, 2], F32, name="weighted")
         ones = keep.tile([P, tiles], F32, name="ones")
@@ -155,18 +155,16 @@ def tile_picked_phnorm_none_p_kernel(tc, x_words, x_scales, w1, gamma, res, offs
                 out=squares[:, c, S:], in_=terms[:, c, :], func=ACT.Identity, scale=unit, bias=distance[c],
                 accum_out=base[c],
             )
+            nc.scalar.activation(
+                out=weighted[:, c], in_=sums[c][:].unsqueeze(1).to_broadcast([P, 2, 2]), func=ACT.Copy,
+                scale=gamma_sb[:, c : c + 1], accum_out=shift[c],
+            )
             nc.scalar.activation(out=rstd[c], in_=second[c], func=ACT.Abs_reciprocal_sqrt, scale=unit, bias=base[c])
 
         def gain(c, cols):
             nc.vector.tensor_scalar(
                 out=gained[c][:, cols], in0=h[c][:, cols], scalar1=gamma_sb[:, c : c + 1], scalar2=GAIN,
                 op0=ALU.mult, op1=ALU.mult,
-            )
-
-        def shifted_mean(c):
-            nc.vector.tensor_scalar(
-                out=weighted[:, c], in0=sums[c][:].unsqueeze(1).to_broadcast([P, 2, 2]),
-                scalar1=gamma_sb[:, c : c + 1], scalar2=None, op0=ALU.mult, op1=ALU.add, accum_out=shift[c],
             )
 
         def finish(c, cols):
@@ -189,11 +187,9 @@ def tile_picked_phnorm_none_p_kernel(tc, x_words, x_scales, w1, gamma, res, offs
             )
             square(c, 1)
             inverse_root(c)
-        shifted_mean(0)
         gain(0, slice(0, S))
+        gain(1, halves[0])
         finish(0, slice(0, S))
-        shifted_mean(1)
-        for cols in halves:
-            gain(1, cols)
+        gain(1, halves[1])
         for cols in halves:
             finish(1, cols)

from contextlib import ExitStack

import concourse.mybir as mybir

K, T, S, N = 512, 2048, 512, 256
FLOPS = 2 * K * S * N

F32 = mybir.dt.float32
BF16 = mybir.dt.bfloat16
I32 = mybir.dt.int32
U32 = mybir.dt.uint32
U16 = mybir.dt.uint16
U8 = mybir.dt.uint8
FP8X4 = mybir.dt.float8_e4m3fn_x4
ALU = mybir.AluOpType
ACT = mybir.ActivationFunctionType

P = 128
PACK = 4
BLOCK_PARTS = 8
QUADRANT = 32
EPS = 1e-5
HALF = S // 2
TERMS = 4
LAP = 8
GAIN = 2.0 * S


def tile_picked_phnorm_none_p_kernel(tc, x_words, x_scales, w1, gamma, res, offs, out):
    nc = tc.nc
    tiles = N // P
    halves = [slice(0, HALF), slice(HALF, S)]
    with ExitStack() as ctx:
        keep = ctx.enter_context(tc.tile_pool(name="keep", bufs=1))
        placed = ctx.enter_context(tc.tile_pool(name="placed", bufs=1))
        psum = ctx.enter_context(tc.psum_pool(name="psum", bufs=1))

        offsets = keep.tile([P, S // 16], U16, name="offsets")
        scale_table = placed.tile([P, T], U8, name="scale_table", offset=0, align_bytes=64)
        nc.vector.memset(scale_table[:].bitcast(I32), 0)

        w_rows = w1.rearrange("(p j) m -> p j m", j=PACK)
        w_raw = [keep.tile([P, PACK, P], F32, name=f"w_raw{c}") for c in range(tiles)]
        word_table = keep.tile([P, T], I32, name="word_table", align_bytes=64)
        nc.sync.dma_start(w_raw[0][:], w_rows[:, :, 0:P])
        nc.sync.dma_start(offsets[:], offs)
        nc.sync.dma_start(scale_table[0:P:BLOCK_PARTS, :].bitcast(I32), x_scales[0].bitcast(I32))
        nc.sync.dma_start(word_table[:], x_words[0].rearrange("p n t -> p (n t)").bitcast(I32))
        nc.sync.dma_start(w_raw[1][:], w_rows[:, :, P : 2 * P])

        warm = keep.tile([P, 2], F32, name="warm")
        nc.vector.memset(warm[:, 0:1], 1.0)
        nc.scalar.activation(out=warm[:, 1:2], in_=warm[:, 0:1], func=ACT.Abs_reciprocal_sqrt)

        res_bytes = HALF * 4
        w_scale = placed.tile([P, N], U8, name="w_scale", offset=0, align_bytes=64)
        gamma_sb = placed.tile([P, tiles], F32, name="gamma_sb", offset=N, align_bytes=64)
        res_at = N + 64
        res_first = placed.tile([P, HALF], F32, name="res_first", offset=res_at, align_bytes=64)
        res_rest = placed.tile([P, 2 * S], F32, name="res_rest", offset=res_at + res_bytes, align_bytes=64)
        res_sb = [[res_first[:], res_rest[:, HALF:S]], [res_rest[:, S : S + HALF], res_rest[:, S + HALF :]]]
        grouped = [keep.tile([P, P, PACK], BF16, name=f"grouped{c}", align_bytes=64) for c in range(tiles)]
        w_codes = [
            keep.tile([P, P], U32, name="w_codes0", align_bytes=64),
            keep.tile([P, P], U32, name="w_codes1", align_bytes=64),
        ]

        def interleave(c):
            nc.scalar.copy(
                out=grouped[c][:].rearrange("p (g i) j -> p g j i", i=PACK),
                in_=w_raw[c][:].rearrange("p j (g i) -> p g j i", i=PACK),
            )

        def quantize(c):
            nc.vector.quantize_mx(
                out=w_codes[c][:].bitcast(FP8X4),
                scales=w_scale[:, c * P : (c + 1) * P],
                in_=grouped[c][:].rearrange("p m j -> p (m j)"),
            )

        x_scale = keep.tile([P, S], U8, name="x_scale", align_bytes=64)
        picked_scales = keep.tile([P, S], U8, name="picked_scales", align_bytes=64)
        nc.vector.memset(x_scale[:].bitcast(I32), 0)
        interleave(0)
        nc.vector.tensor_copy(picked_scales[:], scale_table[:].indirect(offsets[:]))
        for i in range(QUADRANT // BLOCK_PARTS):
            queue = nc.scalar if i % 2 == 0 else nc.sync
            queue.dma_start(
                x_scale[i:P:QUADRANT, :].bitcast(I32),
                picked_scales[BLOCK_PARTS * i : P : QUADRANT, :].bitcast(I32),
            )
        quantize(0)
        for u, cols in enumerate(halves):
            nc.sync.dma_start(res_sb[0][u], res[0:P, cols])
        nc.sync.dma_start(res_rest[:, S:], res[P : 2 * P, :])
        with nc.allow_non_contiguous_dma(reason="one value a channel"):
            nc.sync.dma_start(gamma_sb[:], gamma.rearrange("(c p) o -> p (c o)", p=P))
        interleave(1)

        x_codes = keep.tile([P, S], U32, name="x_codes", align_bytes=64)
        for cols in halves:
            entries = offsets[:, cols.start // 16 : cols.stop // 16]
            nc.vector.tensor_copy(x_codes[:, cols], word_table[:].bitcast(U32).indirect(entries))

        accs = [[psum.tile([P, S], F32, name=f"acc{c}_{u}") for u in range(2)] for c in range(tiles)]
        h = [keep.tile([P, S], F32, name=f"h{c}") for c in range(tiles)]
        gained = [res_rest[:, LAP : S + LAP], keep.tile([P, S], F32, name="gained1")[:]]
        squares = keep.tile([P, tiles, S + TERMS], F32, name="squares")

        def column(name):
            return keep.tile([P, 1], F32, name=name)[:]

        sums = [keep.tile([P, 2], F32, name=f"sums{c}") for c in range(tiles)]
        terms = keep.tile([P, tiles, TERMS], F32, name="terms")
        second = [column(f"second{c}") for c in range(tiles)]
        distance = [squares[:, 1, 0:1], column("distance1")]
        base = [column(f"base{c}") for c in range(tiles)]
        shift = [column(f"shift{c}") for c in range(tiles)]
        rstd = [column(f"rstd{c}") for c in range(tiles)]
        weighted = keep.tile([P, tiles, 2, 2], F32, name="weighted")
        ones = keep.tile([P, tiles], F32, name="ones")
        unit = GAIN * GAIN / (HALF * HALF * S)
        nc.vector.memset(ones[:], 1.0)
        nc.vector.memset(terms[:, :, 2:], 0.0)
        nc.vector.tensor_scalar(
            out=terms[:, :, 1], in0=ones[:], scalar1=EPS * GAIN * GAIN / unit, scalar2=None, op0=ALU.mult,
        )

        def multiply(c):
            for u, cols in enumerate(halves):
                nc.tensor.matmul_mx(
                    out=accs[c][u][:, :HALF],
                    lhsT=w_codes[c][:].bitcast(FP8X4),
                    lhsT_scale=w_scale[:, c * P : (c + 1) * P],
                    rhs=x_codes[:, cols].bitcast(FP8X4),
                    rhs_scale=x_scale[:, cols],
                    start=True,
                    stop=True,
                )

        def add(c, u):
            nc.vector.scalar_tensor_tensor(
                out=h[c][:, halves[u]], in0=accs[c][u][:, :HALF], scalar=1.0, in1=res_sb[c][u],
                op0=ALU.mult, op1=ALU.add, accum_out=sums[c][:, u : u + 1],
            )

        def square(c, u):
            nc.scalar.activation(
                out=squares[:, c, halves[u]], in_=h[c][:, halves[u]], func=ACT.Square, scale=-float(HALF),
                bias=sums[c][:, u : u + 1], accum_out=terms[:, c, 0:1] if u == 0 else second[c],
            )

        def inverse_root(c):
            nc.scalar.activation(
                out=squares[:, c, S:], in_=terms[:, c, :], func=ACT.Identity, scale=unit, bias=distance[c],
                accum_out=base[c],
            )
            nc.scalar.activation(
                out=weighted[:, c], in_=sums[c][:].unsqueeze(1).to_broadcast([P, 2, 2]), func=ACT.Copy,
                scale=gamma_sb[:, c : c + 1], accum_out=shift[c],
            )
            nc.scalar.activation(out=rstd[c], in_=second[c], func=ACT.Abs_reciprocal_sqrt, scale=unit, bias=base[c])

        def gain(c, cols):
            nc.vector.tensor_scalar(
                out=gained[c][:, cols], in0=h[c][:, cols], scalar1=gamma_sb[:, c : c + 1], scalar2=GAIN,
                op0=ALU.mult, op1=ALU.mult,
            )

        def finish(c, cols):
            result = keep.tile([P, cols.stop - cols.start], F32, name=f"result{c}_{cols.start}")
            nc.vector.tensor_scalar(
                out=result[:], in0=gained[c][:, cols], scalar1=shift[c], scalar2=rstd[c],
                op0=ALU.subtract, op1=ALU.mult,
            )
            nc.sync.dma_start(out[c * P : (c + 1) * P, cols], result[:])

        quantize(1)
        for c in range(tiles):
            multiply(c)
        for c in range(tiles):
            add(c, 0)
            square(c, 0)
            add(c, 1)
            nc.scalar.activation(
                out=distance[c], in_=sums[c][:, 1:2], func=ACT.Square, scale=-1.0, bias=sums[c][:, 0:1],
            )
            square(c, 1)
            inverse_root(c)
        gain(0, slice(0, S))
        gain(1, halves[0])
        finish(0, slice(0, S))
        gain(1, halves[1])
        for cols in halves:
            finish(1, cols)
